import numpy as np
import ml_dtypes


def mxq(x, axis, fmt="e4m3"):
    dtype, down = {"e4m3": (ml_dtypes.float8_e4m3fn, 7), "e5m2": (ml_dtypes.float8_e5m2, 14)}[fmt]
    v = np.moveaxis(np.asarray(x, np.float32).astype(ml_dtypes.bfloat16).astype(np.float64), axis, -1)
    blocks = v.reshape(v.shape[:-1] + (-1, 32))
    amax = np.abs(blocks).max(-1, keepdims=True)
    byte = np.maximum(np.where(amax > 0, np.frexp(amax)[1] - 1 + 127, 0) - down, 1)
    scale = np.exp2(byte - 127.0)
    codes = (blocks / scale).astype(np.float32).astype(dtype).astype(np.float64)
    return np.moveaxis((codes * scale).reshape(v.shape), -1, axis)


WIDE = False


def mx_kscale(k):
    if not WIDE:
        return np.ones(k)
    levels = np.array([10, -10, 5, -5, 0])
    if k % 512:
        return np.exp2(np.random.permutation(np.resize(levels, k // 32))).repeat(32)
    a = np.empty((k // 512, 16))
    for p in range(k // 512):
        a[p, :8] = np.random.permutation(np.resize(levels, 8))
        for g in range(8):
            far = levels[np.abs(levels - a[p, g]) >= 10]
            a[p, g + 8] = far[np.random.randint(len(far))]
    return np.exp2(a.ravel()).repeat(32)


def f64(x):
    return np.asarray(x).astype(np.float64)


def striped(idx):
    return np.tile(idx.reshape(-1, 16).T, (8, 1)).astype(np.uint16)


def unstriped(offs):
    return offs[:16].T.reshape(-1).astype(np.int64)


E2M1 = np.array([0.0, 0.5, 1.0, 1.5, 2.0, 3.0, 4.0, 6.0, -0.0, -0.5, -1.0, -1.5, -2.0, -3.0, -4.0, -6.0])


def pack_weight(w, fmt):
    k, n = w.shape
    w = f64(np.asarray(w, np.float32).astype(ml_dtypes.bfloat16)).reshape(k // 32, 32, n)
    amax = np.abs(w).max(1)
    if fmt == "e4m3":
        byte = np.frexp(amax)[1] - 1 + 127 - 7
    else:
        mant, ex = np.frexp(amax / 6.0)
        byte = np.where(mant > 0.5, ex, ex - 1) + 127
    byte = np.clip(np.where(amax > 0, byte, 1), 1, 254)
    scaled = (w * np.exp2(127.0 - byte)[:, None, :]).reshape(k, n).astype(np.float32)
    by_word = np.ascontiguousarray(scaled.reshape(k // 512, 128, 4, n).transpose(0, 1, 3, 2))
    if fmt == "e4m3":
        words = by_word.astype(ml_dtypes.float8_e4m3fn).view(np.uint8)
    else:
        c = by_word.astype(ml_dtypes.float4_e2m1fn).view(np.uint8) & 0xF
        words = (c[..., 0::2] | (c[..., 1::2] << 4)).reshape(k // 512, 128, 2 * n)
    return np.ascontiguousarray(words), np.ascontiguousarray(byte.astype(np.uint8).reshape(k // 512, 16, n))


def unpack_weight(words, scales, fmt):
    g, _, n = scales.shape
    words = np.ascontiguousarray(words).reshape(g, 128, n, -1)
    if fmt == "e4m3":
        vals = words.view(ml_dtypes.float8_e4m3fn).astype(np.float64)
    else:
        nib = np.empty((g, 128, n, 4), np.uint8)
        nib[..., 0::2] = words & 0xF
        nib[..., 1::2] = words >> 4
        vals = E2M1[nib]
    vals = vals * np.repeat(np.exp2(scales.astype(np.float64) - 127.0), 8, axis=1)[..., None]
    return vals.transpose(0, 1, 3, 2).reshape(g * 512, n)


def gelu(v):
    return 0.5 * v * (1.0 + np.tanh(np.sqrt(2.0 / np.pi) * (v + 0.044715 * v**3)))


K, H, N, T, S, T2 = 1536, 1024, 512, 2048, 1024, 2048

def setup_inputs():
    n = np.random.standard_normal
    s = mx_kscale(K)[:, None]
    u = mx_kscale(H)[:, None]
    tab_words, tab_scales = pack_weight(n((K, T)) * s, "e4m3")
    wl_words, wl_scales = pack_weight(n((H, N)) / np.sqrt(H) / u, "e2m1")
    return {
        "tab_words": tab_words, "tab_scales": tab_scales,
        "offs": striped(np.random.permutation(T)[:S]),
        "wp": (n((K, H)) / np.sqrt(K) / s * u.T).astype(np.float32),
        "b": (0.3 * n(H) * u[:, 0]).astype(np.float32),
        "d": (0.5 * np.exp(0.2 * n(H)) / u[:, 0]).astype(np.float32),
        "wl_words": wl_words, "wl_scales": wl_scales,
        "wq": (n((H, N)) / np.sqrt(H) / u).astype(np.float32),
        "c": (0.5 * n(N)).astype(np.float32),
        "wgo": np.exp(0.3 * n((128, S))).astype(np.float32),
        "offs2": striped(np.random.permutation(T2)[:S]),
    }

def reference(tab_words, tab_scales, offs, wp, b, d, wl_words, wl_scales, wq, c, wgo, offs2):
    v = unpack_weight(tab_words, tab_scales, "e4m3")[:, unstriped(offs)]
    wpq = mxq(f64(wp), 0, "e4m3")
    z = (wpq.T @ v) + f64(b)[:, None]
    q = z * z * f64(d)[:, None]
    zq = mxq(z, 0, "e4m3")
    qq = mxq(q, 0, "e4m3")
    wl = unpack_weight(wl_words, wl_scales, "e2m1")
    wqq = mxq(f64(wq), 0, "e4m3")
    y = (wl.T @ zq + wqq.T @ qq) + f64(c)[:, None]
    out = np.zeros((N, T2))
    out[:, unstriped(offs2)] = np.tile(f64(wgo), (N // 128, 1)) * y
    return out

@@ -1,0 +1,292 @@
+from contextlib import ExitStack
+
+import concourse.mybir as mybir
+
+K, H, N, T, S, T2 = 1536, 1024, 512, 2048, 1024, 2048
+FLOPS = 2 * K * H * S + 2 * 2 * H * N * S
+
+F32 = mybir.dt.float32
+BF16 = mybir.dt.bfloat16
+I32 = mybir.dt.int32
+U32 = mybir.dt.uint32
+U16 = mybir.dt.uint16
+U8 = mybir.dt.uint8
+FP8X4 = mybir.dt.float8_e4m3fn_x4
+FP4X4 = mybir.dt.float4_e2m1fn_x4
+ACT = mybir.ActivationFunctionType
+ALU = mybir.AluOpType
+
+P = 128
+KP = 3
+RP = 2
+NT = 4
+CH = 256
+NCH = S // CH
+
+
+def tile_list_quadratic_state_prediction_kernel(
+    tc, tab_words, tab_scales, offs, wp, b, d, wl_words, wl_scales, wq, c, wgo, offs2, out
+):
+    nc = tc.nc
+    with ExitStack() as ctx:
+        lists = ctx.enter_context(tc.tile_pool(name="lists", bufs=1))
+        keep = ctx.enter_context(tc.tile_pool(name="keep", bufs=1))
+        ring = ctx.enter_context(tc.tile_pool(name="ring", bufs=1))
+        psum = ctx.enter_context(tc.psum_pool(name="psum", bufs=1))
+
+        offs_t = lists.tile([P, S // 16], U16, name="offs_t")
+        offs2_t = lists.tile([P, S // 16], U16, name="offs2_t")
+
+        tab_t = [keep.tile([P, T], I32, name="tab_t%d" % a, align_bytes=64) for a in range(KP)]
+        tabsc_t = keep.tile([P, T // 4], I32, name="tabsc_t", align_bytes=64)
+        v_codes = [keep.tile([P, S], U32, name="v_codes%d" % a, align_bytes=64) for a in range(KP)]
+        v_scales = keep.tile([P, S], U8, name="v_scales", align_bytes=64)
+        wl_t = keep.tile([P, RP, 2 * N], U8, name="wl_t", align_bytes=64)
+        wlsc_t = keep.tile([P, RP, N // 4], I32, name="wlsc_t", align_bytes=64)
+        b_t = keep.tile([P, RP, 4], F32, name="b_t")
+        d_t = keep.tile([P, RP, 4], F32, name="d_t")
+        c_t = keep.tile([P, NT], F32, name="c_t")
+        wgo_t = [keep.tile([P, S // 2], F32, name="wgo_t%d" % h) for h in range(2)]
+        out_t = [keep.tile([P, T2], F32, name="out_t%d" % n) for n in range(NT)]
+        wp_codes = {}
+        wp_scales = {}
+        for a in range(RP):
+            for g in range(KP):
+                wp_codes[a, g] = keep.tile([P, 512], U32, name="wp_codes%d%d" % (a, g), align_bytes=64)
+                wp_scales[a, g] = keep.tile([P, 512], U8, name="wp_scales%d%d" % (a, g), align_bytes=64)
+        wq_codes = [keep.tile([P, RP, 256], U32, name="wq_codes%d" % h, align_bytes=64) for h in range(2)]
+        wq_scales = [keep.tile([P, RP, 256], U8, name="wq_scales%d" % h, align_bytes=64) for h in range(2)]
+
+        nc.vector.memset(tabsc_t[:], 0)
+        nc.vector.memset(wlsc_t[:], 0)
+
+        nc.scalar.dma_start(out=d_t[:], in_=d.rearrange("(a p t) -> p a t", a=RP, t=4))
+        tab_scales_i = tab_scales.bitcast(I32)
+        for Q in range(4):
+            nc.scalar.dma_start(out=tabsc_t[32 * Q : 32 * Q + 4 * KP, :], in_=tab_scales_i[:, 4 * Q : 4 * Q + 4, :])
+        nc.scalar.dma_start(out=b_t[:], in_=b.rearrange("(a p t) -> p a t", a=RP, t=4))
+        with nc.allow_non_contiguous_dma(reason="one bias value a partition"):
+            nc.scalar.dma_start(out=c_t[:], in_=c.rearrange("(t p) -> p t", p=P))
+        wl_scales_i = wl_scales.bitcast(I32)
+        for Q in range(4):
+            nc.scalar.dma_start(
+                out=wlsc_t[32 * Q : 32 * Q + 4, :, :],
+                in_=wl_scales_i[:, 4 * Q : 4 * Q + 4, :].rearrange("a r n -> r a n"),
+            )
+
+        wp_raw = {}
+        wq_raw = {}
+
+        def load_tab(g):
+            nc.sync.dma_start(out=tab_t[g][:], in_=tab_words[g].rearrange("p t i -> p (t i)").bitcast(I32))
+
+        def load_wp(a, g):
+            wp_raw[a, g] = ring.tile([P, 4, 512], F32, name="wp_raw", bufs=4)
+            nc.sync.dma_start(
+                out=wp_raw[a, g][:],
+                in_=wp[512 * g : 512 * (g + 1), 512 * a : 512 * (a + 1)].rearrange("(p j) c -> p j c", j=4),
+            )
+
+        def load_wq(h):
+            for a in range(RP):
+                wq_raw[h, a] = ring.tile([P, 4, 256], F32, name="wq_raw", bufs=4)
+                nc.sync.dma_start(
+                    out=wq_raw[h, a][:],
+                    in_=wq[512 * a : 512 * (a + 1), 256 * h : 256 * (h + 1)].rearrange("(p j) c -> p j c", j=4),
+                )
+
+        def copy_on(engine, dst, src):
+            if engine == "V":
+                nc.vector.tensor_copy(out=dst, in_=src)
+            else:
+                nc.scalar.copy(out=dst, in_=src)
+
+        def gather_codes(g, lo, hi):
+            nc.vector.tensor_copy(
+                out=v_codes[g][:, lo:hi], in_=tab_t[g][:].bitcast(U32).indirect(offs_t[:, lo // 16 : hi // 16])
+            )
+
+        def quantise_wp(a, g, engine):
+            grouped = ring.tile([P, 4, P, 4], BF16, name="w_grouped", bufs=3, align_bytes=64)
+            copy_on(
+                engine,
+                grouped[:].rearrange("p t m j -> p m j t"),
+                wp_raw[a, g][:].rearrange("p j (m t) -> p m j t", t=4),
+            )
+            nc.vector.quantize_mx(
+                out=wp_codes[a, g][:].bitcast(FP8X4),
+                scales=wp_scales[a, g][:],
+                in_=grouped[:].rearrange("p t m j -> p (t m j)"),
+            )
+
+        def quantise_wq(h, engine):
+            grouped = ring.tile([P, RP, 256, 4], BF16, name="w_grouped", bufs=3, align_bytes=64)
+            for a in range(RP):
+                copy_on(
+                    engine,
+                    grouped[:, a].rearrange("p (c i) j -> p c j i", i=4),
+                    wq_raw[h, a][:].rearrange("p j (c i) -> p c j i", i=4),
+                )
+            nc.vector.quantize_mx(
+                out=wq_codes[h][:].rearrange("p a n -> p (a n)").bitcast(FP8X4),
+                scales=wq_scales[h][:].rearrange("p a n -> p (a n)"),
+                in_=grouped[:].rearrange("p a n j -> p (a n j)"),
+            )
+
+        zq_codes = {}
+        zq_scales = {}
+
+        def z_pass(acc, a, t, g, ch):
+            tok = slice(CH * ch, CH * (ch + 1))
+            cols = slice(P * t, P * (t + 1))
+            nc.tensor.matmul_mx(
+                out=acc,
+                lhsT=wp_codes[a, g][:, cols].bitcast(FP8X4),
+                lhsT_scale=wp_scales[a, g][:, cols],
+                rhs=v_codes[g][:, tok].bitcast(FP8X4),
+                rhs_scale=v_scales[4 * g : P, tok],
+                start=(g == 0),
+                stop=(g == KP - 1),
+            )
+
+        def make_zq(a, ch, engines, spread):
+            if spread:
+                banks = [psum.tile([P, 2, CH], F32, name="z_bank", bufs=6) for t in range(4)]
+                accs = [banks[t][:, 0, :] for t in range(4)]
+                for g in range(KP):
+                    for t in range(4):
+                        z_pass(accs[t], a, t, g, ch)
+            else:
+                banks = [psum.tile([P, 2, CH], F32, name="z_bank", bufs=6) for u in range(2)]
+                accs = [banks[t // 2][:, t % 2, :] for t in range(4)]
+                for t in range(4):
+                    for g in range(KP):
+                        z_pass(accs[t], a, t, g, ch)
+            for s in range(2):
+                rows = ring.tile([P, 4, CH], BF16, name="zq_rows", bufs=6)
+                for t in range(4):
+                    if s == 0:
+                        nc.scalar.activation(out=rows[:, t, :], in_=accs[t], func=ACT.Identity, bias=b_t[:, a, t : t + 1])
+                    else:
+                        nc.scalar.activation(
+                            out=rows[:, t, :],
+                            in_=accs[t],
+                            func=ACT.Square,
+                            bias=rootb_t[:, a, t : t + 1],
+                            scale=root_t[:, a, t : t + 1],
+                        )
+                grouped = ring.tile([P, CH, 4], BF16, name="zq_grouped", bufs=6, align_bytes=64)
+                copy_on(
+                    engines[s],
+                    grouped[:].rearrange("p (c i) t -> p c t i", i=4),
+                    rows[:].rearrange("p t (c i) -> p c t i", i=4),
+                )
+                zq_codes[s, a, ch] = ring.tile([P, CH], U32, name="zq_codes", bufs=10, align_bytes=64)
+                zq_scales[s, a, ch] = ring.tile([P, CH], U8, name="zq_scales", bufs=10, align_bytes=64)
+                nc.vector.quantize_mx(
+                    out=zq_codes[s, a, ch][:].bitcast(FP8X4),
+                    scales=zq_scales[s, a, ch][:],
+                    in_=grouped[:].rearrange("p n t -> p (n t)"),
+                )
+
+        y_t = {}
+
+        def make_y(ch, n):
+            bank = psum.tile([P, CH], F32, name="y_bank", bufs=2)
+            h, m = divmod(n, 2)
+            for u in range(CH // P):
+                tok = slice(P * u, P * (u + 1))
+                for a in range(RP):
+                    nc.tensor.matmul_mx(
+                        out=bank[:, tok],
+                        lhsT=wl_t[:, a, 2 * P * n : 2 * P * (n + 1)].bitcast(FP4X4),
+                        lhsT_scale=wlsc_t[:, a, :].bitcast(U8)[:, P * n : P * (n + 1)],
+                        rhs=zq_codes[0, a, ch][:, tok].bitcast(FP8X4),
+                        rhs_scale=zq_scales[0, a, ch][:, tok],
+                        start=(a == 0),
+                        stop=False,
+                    )
+                for a in range(RP):
+                    nc.tensor.matmul_mx(
+                        out=bank[:, tok],
+                        lhsT=wq_codes[h][:, a, P * m : P * (m + 1)].bitcast(FP8X4),
+                        lhsT_scale=wq_scales[h][:, a, P * m : P * (m + 1)],
+                        rhs=zq_codes[1, a, ch][:, tok].bitcast(FP8X4),
+                        rhs_scale=zq_scales[1, a, ch][:, tok],
+                        start=False,
+                        stop=(a == RP - 1),
+                    )
+            y_t[ch, n] = ring.tile([P, CH], F32, name="y_t", bufs=8)
+            nc.scalar.activation(out=y_t[ch, n][:], in_=bank[:], func=ACT.Identity, bias=c_t[:, n : n + 1])
+
+        def scatter(ch, n):
+            h, u = divmod(ch, 2)
+            nc.vector.tensor_tensor(
+                out=out_t[n][:].indirect(offs2_t[:, CH * ch // 16 : CH * (ch + 1) // 16]),
+                in0=y_t[ch, n][:],
+                in1=wgo_t[h][:, CH * u : CH * (u + 1)],
+                op=ALU.mult,
+            )
+
+        nc.sync.dma_start(offs_t[:], offs)
+        load_tab(0)
+        load_wp(0, 0)
+        load_wp(0, 1)
+        load_tab(1)
+        load_wp(0, 2)
+        load_tab(2)
+
+        root0_t = keep.tile([P, RP, 4], F32, name="root0_t")
+        quot_t = keep.tile([P, RP, 4], F32, name="quot_t")
+        root_t = keep.tile([P, RP, 4], F32, name="root_t")
+        rootb_t = keep.tile([P, RP, 4], F32, name="rootb_t")
+        nc.scalar.activation(out=root0_t[:], in_=d_t[:], func=ACT.Sqrt)
+        nc.vector.reciprocal(out=quot_t[:], in_=root0_t[:])
+        nc.vector.tensor_tensor(out=quot_t[:], in0=quot_t[:], in1=d_t[:], op=ALU.mult)
+        nc.vector.tensor_tensor(out=quot_t[:], in0=quot_t[:], in1=root0_t[:], op=ALU.add)
+        nc.vector.tensor_scalar(out=root_t[:], in0=quot_t[:], scalar1=0.5, scalar2=None, op0=ALU.mult)
+        nc.vector.tensor_tensor(out=rootb_t[:], in0=root_t[:], in1=b_t[:], op=ALU.mult)
+
+        gather_codes(0, 0, S)
+        quantise_wp(0, 0, "S")
+        nc.vector.tensor_copy(out=v_scales[:], in_=tabsc_t[:].bitcast(U8).indirect(offs_t[:]))
+        quantise_wp(0, 1, "S")
+        load_wp(1, 0)
+        load_wp(1, 1)
+        gather_codes(1, 0, S)
+        quantise_wp(0, 2, "S")
+        load_wp(1, 2)
+        nc.sync.dma_start(out=wl_t[:].bitcast(I32), in_=wl_words.rearrange("a p n -> p a n").bitcast(I32))
+        load_wq(0)
+        nc.sync.dma_start(offs2_t[:], offs2)
+        nc.sync.dma_start(out=wgo_t[0][:], in_=wgo[:, 0 : S // 2])
+        load_wq(1)
+        nc.sync.dma_start(out=wgo_t[1][:], in_=wgo[:, S // 2 : S])
+
+        gather_codes(2, 0, CH)
+        gather_codes(2, CH, S)
+        quantise_wp(1, 0, "V")
+        quantise_wp(1, 1, "V")
+        quantise_wp(1, 2, "V")
+        make_zq(0, 0, "SS", False)
+        make_zq(1, 0, "VV", True)
+        quantise_wq(0, "V")
+        make_y(0, 0)
+        make_y(0, 1)
+        quantise_wq(1, "S")
+        make_y(0, 2)
+        make_y(0, 3)
+        for n in range(NT):
+            nc.vector.memset(out_t[n][:], 0.0)
+        for ch in range(1, NCH):
+            make_zq(0, ch, "VS" if ch == NCH - 1 else "SS", False)
+            make_zq(1, ch, "VS", False)
+            if ch < NCH - 1:
+                for n in range(NT):
+                    scatter(ch - 1, n)
+            for n in range(NT):
+                make_y(ch, n)
+        for n in range(NT):
+            scatter(NCH - 2, n)
+            scatter(NCH - 1, n)
+            nc.sync.dma_start(out=out[P * n : P * (n + 1), :], in_=out_t[n][:])

@@ -20,8 +20,8 @@ P = 128
 KP = 3
 RP = 2
 NT = 4
-CH = 256
-NCH = S // CH
+LOADS = "offs offs2 t02 p00 t24 d c t11 A1 A0 b B0 A2 B1 p01 A3 B3 B2 p02 L2 p11 L1 p10 L3 p12 L0 wl o1 q0 q1 o0"
+PLAN = "g041 p00V g040 p10V p02S p01S g042 p12V G04 z010VS32 p11V z120VV73 z011VV4501 z121VS35 w000VV y0106 y0115 z231VS73 w001VV y0125 s012 s010 s011 y1200 y1221 y0136 z230VS47 y1235 s120 z340SS61 y1213 z341VS27 s013 s123 y2321 y2303 y2317 y3425 y3417 s121 s231 s341 o001 y2336 y3406 y3437 s122 s230 s340 o000 s232 s343 s233 o003 s342 o002"
 
 
 def tile_list_quadratic_state_prediction_kernel(
@@ -46,7 +46,7 @@ def tile_list_quadratic_state_prediction_kernel(
         b_t = keep.tile([P, RP, 4], F32, name="b_t")
         d_t = keep.tile([P, RP, 4], F32, name="d_t")
         c_t = keep.tile([P, NT], F32, name="c_t")
-        wgo_t = [keep.tile([P, S // 2], F32, name="wgo_t%d" % h) for h in range(2)]
+        wgo_t = keep.tile([P, S], F32, name="wgo_t")
         out_t = [keep.tile([P, T2], F32, name="out_t%d" % n) for n in range(NT)]
         wp_codes = {}
         wp_scales = {}
@@ -57,31 +57,23 @@ def tile_list_quadratic_state_prediction_kernel(
         wq_codes = [keep.tile([P, RP, 256], U32, name="wq_codes%d" % h, align_bytes=64) for h in range(2)]
         wq_scales = [keep.tile([P, RP, 256], U8, name="wq_scales%d" % h, align_bytes=64) for h in range(2)]
 
-        nc.vector.memset(tabsc_t[:], 0)
-        nc.vector.memset(wlsc_t[:], 0)
+        nc.vector.memset(tabsc_t[:, 0:256], 0)
+        nc.gpsimd.memset(tabsc_t[:, 256:512], 0)
+        nc.gpsimd.memset(wlsc_t[:], 0)
 
-        nc.scalar.dma_start(out=d_t[:], in_=d.rearrange("(a p t) -> p a t", a=RP, t=4))
         tab_scales_i = tab_scales.bitcast(I32)
-        for Q in range(4):
-            nc.scalar.dma_start(out=tabsc_t[32 * Q : 32 * Q + 4 * KP, :], in_=tab_scales_i[:, 4 * Q : 4 * Q + 4, :])
-        nc.scalar.dma_start(out=b_t[:], in_=b.rearrange("(a p t) -> p a t", a=RP, t=4))
-        with nc.allow_non_contiguous_dma(reason="one bias value a partition"):
-            nc.scalar.dma_start(out=c_t[:], in_=c.rearrange("(t p) -> p t", p=P))
         wl_scales_i = wl_scales.bitcast(I32)
-        for Q in range(4):
-            nc.scalar.dma_start(
-                out=wlsc_t[32 * Q : 32 * Q + 4, :, :],
-                in_=wl_scales_i[:, 4 * Q : 4 * Q + 4, :].rearrange("a r n -> r a n"),
-            )
 
         wp_raw = {}
         wq_raw = {}
 
-        def load_tab(g):
-            nc.sync.dma_start(out=tab_t[g][:], in_=tab_words[g].rearrange("p t i -> p (t i)").bitcast(I32))
+        def load_tab(g, pieces):
+            words = tab_words[g].rearrange("p t i -> p (t i)").bitcast(I32)
+            for lo in range(0, T, T // pieces):
+                nc.sync.dma_start(out=tab_t[g][:, lo : lo + T // pieces], in_=words[:, lo : lo + T // pieces])
 
         def load_wp(a, g):
-            wp_raw[a, g] = ring.tile([P, 4, 512], F32, name="wp_raw", bufs=4)
+            wp_raw[a, g] = ring.tile([P, 4, 512], F32, name="wp_raw", tag="stage", bufs=8, align_bytes=64)
             nc.sync.dma_start(
                 out=wp_raw[a, g][:],
                 in_=wp[512 * g : 512 * (g + 1), 512 * a : 512 * (a + 1)].rearrange("(p j) c -> p j c", j=4),
@@ -108,11 +100,13 @@ def tile_list_quadratic_state_prediction_kernel(
 
         def quantise_wp(a, g, engine):
             grouped = ring.tile([P, 4, P, 4], BF16, name="w_grouped", bufs=3, align_bytes=64)
-            copy_on(
-                engine,
-                grouped[:].rearrange("p t m j -> p m j t"),
-                wp_raw[a, g][:].rearrange("p j (m t) -> p m j t", t=4),
-            )
+            dst = grouped[:].rearrange("p t m j -> p m j t")
+            src = wp_raw[a, g][:].rearrange("p j (m t) -> p m j t", t=4)
+            if engine == "H":
+                copy_on("V", dst[:, 0:80], src[:, 0:80])
+                copy_on("S", dst[:, 80:P], src[:, 80:P])
+            else:
+                copy_on(engine, dst, src)
             nc.vector.quantize_mx(
                 out=wp_codes[a, g][:].bitcast(FP8X4),
                 scales=wp_scales[a, g][:],
@@ -123,7 +117,7 @@ def tile_list_quadratic_state_prediction_kernel(
             grouped = ring.tile([P, RP, 256, 4], BF16, name="w_grouped", bufs=3, align_bytes=64)
             for a in range(RP):
                 copy_on(
-                    engine,
+                    engine[a],
                     grouped[:, a].rearrange("p (c i) j -> p c j i", i=4),
                     wq_raw[h, a][:].rearrange("p j (c i) -> p c j i", i=4),
                 )
@@ -136,105 +130,151 @@ def tile_list_quadratic_state_prediction_kernel(
         zq_codes = {}
         zq_scales = {}
 
-        def z_pass(acc, a, t, g, ch):
-            tok = slice(CH * ch, CH * (ch + 1))
+        def z_pass(acc, a, t, g, lo, hi):
             cols = slice(P * t, P * (t + 1))
             nc.tensor.matmul_mx(
                 out=acc,
                 lhsT=wp_codes[a, g][:, cols].bitcast(FP8X4),
                 lhsT_scale=wp_scales[a, g][:, cols],
-                rhs=v_codes[g][:, tok].bitcast(FP8X4),
-                rhs_scale=v_scales[4 * g : P, tok],
+                rhs=v_codes[g][:, lo:hi].bitcast(FP8X4),
+                rhs_scale=v_scales[4 * g : P, lo:hi],
                 start=(g == 0),
                 stop=(g == KP - 1),
             )
 
-        def make_zq(a, ch, engines, spread):
+        bank_t = [psum.tile([P, 512], F32, name="bank%d" % u) for u in range(8)]
+
+        def make_zq(a, lo, hi, engines, which):
+            width = hi - lo
+            banks = [bank_t[int(u)] for u in which]
+            spread = width == 256 and len(banks) == 4
             if spread:
-                banks = [psum.tile([P, 2, CH], F32, name="z_bank", bufs=6) for t in range(4)]
-                accs = [banks[t][:, 0, :] for t in range(4)]
+                accs = [banks[t][:, 0:width] for t in range(4)]
                 for g in range(KP):
                     for t in range(4):
-                        z_pass(accs[t], a, t, g, ch)
+                        z_pass(accs[t], a, t, g, lo, hi)
             else:
-                banks = [psum.tile([P, 2, CH], F32, name="z_bank", bufs=6) for u in range(2)]
-                accs = [banks[t // 2][:, t % 2, :] for t in range(4)]
+                per_bank = 512 // width
+                accs = [banks[t // per_bank][:, width * (t % per_bank) : width * (t % per_bank + 1)] for t in range(4)]
                 for t in range(4):
                     for g in range(KP):
-                        z_pass(accs[t], a, t, g, ch)
+                        z_pass(accs[t], a, t, g, lo, hi)
+            rows = ring.tile([P, 2, 4, width], BF16, name="zq_rows", tag="stage", bufs=8, align_bytes=64)
+            for s, t in (
+                [(s, t) for s in range(2) for t in range(4)] if spread else [(s, t) for t in range(4) for s in range(2)]
+            ):
+                if s == 0:
+                    nc.scalar.activation(out=rows[:, s, t, :], in_=accs[t], func=ACT.Identity, bias=b_t[:, a, t : t + 1])
+                else:
+                    nc.scalar.activation(
+                        out=rows[:, s, t, :],
+                        in_=accs[t],
+                        func=ACT.Square,
+                        bias=rootb_t[:, a, t : t + 1],
+                        scale=root_t[:, a, t : t + 1],
+                    )
+            grouped = ring.tile([P, 2, width, 4], BF16, name="zq_grouped", tag="stage", bufs=8, align_bytes=64)
             for s in range(2):
-                rows = ring.tile([P, 4, CH], BF16, name="zq_rows", bufs=6)
-                for t in range(4):
-                    if s == 0:
-                        nc.scalar.activation(out=rows[:, t, :], in_=accs[t], func=ACT.Identity, bias=b_t[:, a, t : t + 1])
-                    else:
-                        nc.scalar.activation(
-                            out=rows[:, t, :],
-                            in_=accs[t],
-                            func=ACT.Square,
-                            bias=rootb_t[:, a, t : t + 1],
-                            scale=root_t[:, a, t : t + 1],
-                        )
-                grouped = ring.tile([P, CH, 4], BF16, name="zq_grouped", bufs=6, align_bytes=64)
                 copy_on(
                     engines[s],
-                    grouped[:].rearrange("p (c i) t -> p c t i", i=4),
-                    rows[:].rearrange("p t (c i) -> p c t i", i=4),
+                    grouped[:, s].rearrange("p (c i) t -> p c t i", i=4),
+                    rows[:, s].rearrange("p t (c i) -> p c t i", i=4),
                 )
-                zq_codes[s, a, ch] = ring.tile([P, CH], U32, name="zq_codes", bufs=10, align_bytes=64)
-                zq_scales[s, a, ch] = ring.tile([P, CH], U8, name="zq_scales", bufs=10, align_bytes=64)
                 nc.vector.quantize_mx(
-                    out=zq_codes[s, a, ch][:].bitcast(FP8X4),
-                    scales=zq_scales[s, a, ch][:],
-                    in_=grouped[:].rearrange("p n t -> p (n t)"),
+                    out=zq_codes[s, a][:, lo:hi].bitcast(FP8X4),
+                    scales=zq_scales[s, a][:, lo:hi],
+                    in_=grouped[:, s].rearrange("p n t -> p (n t)"),
                 )
+
+        for s in range(2):
+            for a in range(RP):
+                zq_codes[s, a] = keep.tile([P, S], U32, name="zq_codes%d%d" % (s, a), align_bytes=64)
+                zq_scales[s, a] = keep.tile([P, S], U8, name="zq_scales%d%d" % (s, a), align_bytes=64)
 
         y_t = {}
 
-        def make_y(ch, n):
-            bank = psum.tile([P, CH], F32, name="y_bank", bufs=2)
+        def make_y(lo, hi, n, which):
+            width = hi - lo
+            step = 512 if width == 512 else P
+            bank = bank_t[which]
             h, m = divmod(n, 2)
-            for u in range(CH // P):
-                tok = slice(P * u, P * (u + 1))
+            for u in range(0, width, step):
+                tok = slice(lo + u, lo + u + step)
                 for a in range(RP):
                     nc.tensor.matmul_mx(
-                        out=bank[:, tok],
+                        out=bank[:, u : u + step],
                         lhsT=wl_t[:, a, 2 * P * n : 2 * P * (n + 1)].bitcast(FP4X4),
                         lhsT_scale=wlsc_t[:, a, :].bitcast(U8)[:, P * n : P * (n + 1)],
-                        rhs=zq_codes[0, a, ch][:, tok].bitcast(FP8X4),
-                        rhs_scale=zq_scales[0, a, ch][:, tok],
+                        rhs=zq_codes[0, a][:, tok].bitcast(FP8X4),
+                        rhs_scale=zq_scales[0, a][:, tok],
                         start=(a == 0),
                         stop=False,
                     )
                 for a in range(RP):
                     nc.tensor.matmul_mx(
-                        out=bank[:, tok],
+                        out=bank[:, u : u + step],
                         lhsT=wq_codes[h][:, a, P * m : P * (m + 1)].bitcast(FP8X4),
                         lhsT_scale=wq_scales[h][:, a, P * m : P * (m + 1)],
-                        rhs=zq_codes[1, a, ch][:, tok].bitcast(FP8X4),
-                        rhs_scale=zq_scales[1, a, ch][:, tok],
+                        rhs=zq_codes[1, a][:, tok].bitcast(FP8X4),
+                        rhs_scale=zq_scales[1, a][:, tok],
                         start=False,
                         stop=(a == RP - 1),
                     )
-            y_t[ch, n] = ring.tile([P, CH], F32, name="y_t", bufs=8)
-            nc.scalar.activation(out=y_t[ch, n][:], in_=bank[:], func=ACT.Identity, bias=c_t[:, n : n + 1])
+            y_t[lo, n] = ring.tile([P, width], F32, name="y_t", bufs=6)
+            nc.scalar.activation(out=y_t[lo, n][:], in_=bank[:, 0:width], func=ACT.Identity, bias=c_t[:, n : n + 1])
 
-        def scatter(ch, n):
-            h, u = divmod(ch, 2)
+        def scatter(lo, hi, n):
             nc.vector.tensor_tensor(
-                out=out_t[n][:].indirect(offs2_t[:, CH * ch // 16 : CH * (ch + 1) // 16]),
-                in0=y_t[ch, n][:],
-                in1=wgo_t[h][:, CH * u : CH * (u + 1)],
+                out=out_t[n][:].indirect(offs2_t[:, lo // 16 : hi // 16]),
+                in0=y_t[lo, n][:],
+                in1=wgo_t[:, lo:hi],
                 op=ALU.mult,
             )
 
-        nc.sync.dma_start(offs_t[:], offs)
-        load_tab(0)
-        load_wp(0, 0)
-        load_wp(0, 1)
-        load_tab(1)
-        load_wp(0, 2)
-        load_tab(2)
+        nc.vector.memset(out_t[0][:], 0.0)
+        nc.vector.memset(out_t[1][:], 0.0)
+        nc.gpsimd.memset(out_t[2][:], 0.0)
+        nc.gpsimd.memset(out_t[3][:], 0.0)
+
+        for step in LOADS.split():
+            if step == "offs":
+                nc.sync.dma_start(offs_t[:], offs)
+            elif step == "offs2":
+                nc.sync.dma_start(offs2_t[:], offs2)
+            elif step == "d":
+                nc.sync.dma_start(out=d_t[:], in_=d.rearrange("(a p t) -> p a t", a=RP, t=4))
+            elif step == "b":
+                nc.sync.dma_start(out=b_t[:], in_=b.rearrange("(a p t) -> p a t", a=RP, t=4))
+            elif step == "c":
+                with nc.allow_non_contiguous_dma(reason="one bias value a partition"):
+                    nc.sync.dma_start(out=c_t[:], in_=c.rearrange("(t p) -> p t", p=P))
+            elif step == "wl":
+                nc.sync.dma_start(out=wl_t[:].bitcast(I32), in_=wl_words.rearrange("a p n -> p a n").bitcast(I32))
+            elif step[0] == "T":
+                Q = int(step[1])
+                nc.sync.dma_start(out=tabsc_t[32 * Q : 32 * Q + 4 * KP, :], in_=tab_scales_i[:, 4 * Q : 4 * Q + 4, :])
+            elif step[0] == "A":
+                Q = int(step[1])
+                nc.sync.dma_start(out=tabsc_t[32 * Q : 32 * Q + 8, :], in_=tab_scales_i[0:2, 4 * Q : 4 * Q + 4, :])
+            elif step[0] == "B":
+                Q = int(step[1])
+                nc.sync.dma_start(out=tabsc_t[32 * Q + 8 : 32 * Q + 12, :], in_=tab_scales_i[2, 4 * Q : 4 * Q + 4, :])
+            elif step[0] == "L":
+                Q = int(step[1])
+                nc.sync.dma_start(
+                    out=wlsc_t[32 * Q : 32 * Q + 4, :, :],
+                    in_=wl_scales_i[:, 4 * Q : 4 * Q + 4, :].rearrange("a r n -> r a n"),
+                )
+            elif step[0] == "t":
+                load_tab(int(step[1]), int(step[2]))
+            elif step[0] == "p":
+                load_wp(int(step[1]), int(step[2]))
+            elif step[0] == "q":
+                load_wq(int(step[1]))
+            else:
+                h = int(step[1])
+                cols = slice(S // 2 * h, S // 2 * (h + 1))
+                nc.sync.dma_start(out=wgo_t[:, cols], in_=wgo[:, cols])
 
         root0_t = keep.tile([P, RP, 4], F32, name="root0_t")
         quot_t = keep.tile([P, RP, 4], F32, name="quot_t")
@@ -247,46 +287,27 @@ def tile_list_quadratic_state_prediction_kernel(
         nc.vector.tensor_scalar(out=root_t[:], in0=quot_t[:], scalar1=0.5, scalar2=None, op0=ALU.mult)
         nc.vector.tensor_tensor(out=rootb_t[:], in0=root_t[:], in1=b_t[:], op=ALU.mult)
 
-        gather_codes(0, 0, S)
-        quantise_wp(0, 0, "S")
-        nc.vector.tensor_copy(out=v_scales[:], in_=tabsc_t[:].bitcast(U8).indirect(offs_t[:]))
-        quantise_wp(0, 1, "S")
-        load_wp(1, 0)
-        load_wp(1, 1)
-        gather_codes(1, 0, S)
-        quantise_wp(0, 2, "S")
-        load_wp(1, 2)
-        nc.sync.dma_start(out=wl_t[:].bitcast(I32), in_=wl_words.rearrange("a p n -> p a n").bitcast(I32))
-        load_wq(0)
-        nc.sync.dma_start(offs2_t[:], offs2)
-        nc.sync.dma_start(out=wgo_t[0][:], in_=wgo[:, 0 : S // 2])
-        load_wq(1)
-        nc.sync.dma_start(out=wgo_t[1][:], in_=wgo[:, S // 2 : S])
-
-        gather_codes(2, 0, CH)
-        gather_codes(2, CH, S)
-        quantise_wp(1, 0, "V")
-        quantise_wp(1, 1, "V")
-        quantise_wp(1, 2, "V")
-        make_zq(0, 0, "SS", False)
-        make_zq(1, 0, "VV", True)
-        quantise_wq(0, "V")
-        make_y(0, 0)
-        make_y(0, 1)
-        quantise_wq(1, "S")
-        make_y(0, 2)
-        make_y(0, 3)
-        for n in range(NT):
-            nc.vector.memset(out_t[n][:], 0.0)
-        for ch in range(1, NCH):
-            make_zq(0, ch, "VS" if ch == NCH - 1 else "SS", False)
-            make_zq(1, ch, "VS", False)
-            if ch < NCH - 1:
-                for n in range(NT):
-                    scatter(ch - 1, n)
-            for n in range(NT):
-                make_y(ch, n)
-        for n in range(NT):
-            scatter(NCH - 2, n)
-            scatter(NCH - 1, n)
-            nc.sync.dma_start(out=out[P * n : P * (n + 1), :], in_=out_t[n][:])
+        for step in PLAN.split():
+            kind = step[0]
+            lo = 256 * int(step[1])
+            hi = 256 * int(step[2])
+            if kind == "g":
+                gather_codes(int(step[3]), lo, hi)
+            elif kind == "G":
+                nc.vector.tensor_copy(
+                    out=v_scales[:, lo:hi], in_=tabsc_t[:].bitcast(U8).indirect(offs_t[:, lo // 16 : hi // 16])
+                )
+            elif kind == "p":
+                quantise_wp(int(step[1]), int(step[2]), step[3])
+            elif kind == "z":
+                make_zq(int(step[3]), lo, hi, step[4:6], step[6:])
+            elif kind == "w":
+                quantise_wq(int(step[3]), step[4:6])
+            elif kind == "y":
+                make_y(lo, hi, int(step[3]), int(step[4]))
+            elif kind == "s":
+                for n in step[3:]:
+                    scatter(lo, hi, int(n))
+            else:
+                n = int(step[3])
+                nc.sync.dma_start(out=out[P * n : P * (n + 1), :], in_=out_t[n][:])

@@ -20,8 +20,7 @@ P = 128
 KP = 3
 RP = 2
 NT = 4
-LOADS = "offs offs2 t02 p00 t24 d c t11 A1 A0 b B0 A2 B1 p01 A3 B3 B2 p02 L2 p11 L1 p10 L3 p12 L0 wl o1 q0 q1 o0"
-PLAN = "g041 p00V g040 p10V p02S p01S g042 p12V G04 z010VS32 p11V z120VV73 z011VV4501 z121VS35 w000VV y0106 y0115 z231VS73 w001VV y0125 s012 s010 s011 y1200 y1221 y0136 z230VS47 y1235 s120 z340SS61 y1213 z341VS27 s013 s123 y2321 y2303 y2317 y3425 y3417 s121 s231 s341 o001 y2336 y3406 y3437 s122 s230 s340 o000 s232 s343 s233 o003 s342 o002"
+CHUNK = 256
 
 
 def tile_list_quadratic_state_prediction_kernel(
@@ -37,9 +36,9 @@ def tile_list_quadratic_state_prediction_kernel(
         offs_t = lists.tile([P, S // 16], U16, name="offs_t")
         offs2_t = lists.tile([P, S // 16], U16, name="offs2_t")
 
-        tab_t = [keep.tile([P, T], I32, name="tab_t%d" % a, align_bytes=64) for a in range(KP)]
+        tab_t = [keep.tile([P, T], I32, name="tab_t%d" % g, align_bytes=64) for g in range(KP)]
         tabsc_t = keep.tile([P, T // 4], I32, name="tabsc_t", align_bytes=64)
-        v_codes = [keep.tile([P, S], U32, name="v_codes%d" % a, align_bytes=64) for a in range(KP)]
+        v_codes = [keep.tile([P, S], U32, name="v_codes%d" % g, align_bytes=64) for g in range(KP)]
         v_scales = keep.tile([P, S], U8, name="v_scales", align_bytes=64)
         wl_t = keep.tile([P, RP, 2 * N], U8, name="wl_t", align_bytes=64)
         wlsc_t = keep.tile([P, RP, N // 4], I32, name="wlsc_t", align_bytes=64)
@@ -48,32 +47,34 @@ def tile_list_quadratic_state_prediction_kernel(
         c_t = keep.tile([P, NT], F32, name="c_t")
         wgo_t = keep.tile([P, S], F32, name="wgo_t")
         out_t = [keep.tile([P, T2], F32, name="out_t%d" % n) for n in range(NT)]
+        wp_raw = {}
         wp_codes = {}
         wp_scales = {}
         for a in range(RP):
             for g in range(KP):
+                wp_raw[a, g] = keep.tile([P, 4, 512], F32, name="wp_raw%d%d" % (a, g))
                 wp_codes[a, g] = keep.tile([P, 512], U32, name="wp_codes%d%d" % (a, g), align_bytes=64)
                 wp_scales[a, g] = keep.tile([P, 512], U8, name="wp_scales%d%d" % (a, g), align_bytes=64)
+        wq_raw = {}
+        for h in range(2):
+            for a in range(RP):
+                wq_raw[h, a] = keep.tile([P, 4, 256], F32, name="wq_raw%d%d" % (h, a))
         wq_codes = [keep.tile([P, RP, 256], U32, name="wq_codes%d" % h, align_bytes=64) for h in range(2)]
         wq_scales = [keep.tile([P, RP, 256], U8, name="wq_scales%d" % h, align_bytes=64) for h in range(2)]
-
-        nc.vector.memset(tabsc_t[:, 0:256], 0)
-        nc.gpsimd.memset(tabsc_t[:, 256:512], 0)
-        nc.gpsimd.memset(wlsc_t[:], 0)
+        zq_codes = {}
+        zq_scales = {}
+        for s in range(2):
+            for a in range(RP):
+                zq_codes[s, a] = keep.tile([P, S], U32, name="zq_codes%d%d" % (s, a), align_bytes=64)
+                zq_scales[s, a] = keep.tile([P, S], U8, name="zq_scales%d%d" % (s, a), align_bytes=64)
 
         tab_scales_i = tab_scales.bitcast(I32)
         wl_scales_i = wl_scales.bitcast(I32)
 
-        wp_raw = {}
-        wq_raw = {}
-
-        def load_tab(g, pieces):
-            words = tab_words[g].rearrange("p t i -> p (t i)").bitcast(I32)
-            for lo in range(0, T, T // pieces):
-                nc.sync.dma_start(out=tab_t[g][:, lo : lo + T // pieces], in_=words[:, lo : lo + T // pieces])
+        def load_tab(g):
+            nc.sync.dma_start(out=tab_t[g][:], in_=tab_words[g].rearrange("p t i -> p (t i)").bitcast(I32))
 
         def load_wp(a, g):
-            wp_raw[a, g] = ring.tile([P, 4, 512], F32, name="wp_raw", tag="stage", bufs=8, align_bytes=64)
             nc.sync.dma_start(
                 out=wp_raw[a, g][:],
                 in_=wp[512 * g : 512 * (g + 1), 512 * a : 512 * (a + 1)].rearrange("(p j) c -> p j c", j=4),
@@ -81,45 +82,53 @@ def tile_list_quadratic_state_prediction_kernel(
 
         def load_wq(h):
             for a in range(RP):
-                wq_raw[h, a] = ring.tile([P, 4, 256], F32, name="wq_raw", bufs=4)
                 nc.sync.dma_start(
                     out=wq_raw[h, a][:],
                     in_=wq[512 * a : 512 * (a + 1), 256 * h : 256 * (h + 1)].rearrange("(p j) c -> p j c", j=4),
                 )
 
-        def copy_on(engine, dst, src):
-            if engine == "V":
-                nc.vector.tensor_copy(out=dst, in_=src)
-            else:
-                nc.scalar.copy(out=dst, in_=src)
+        def load_wl_scales(q):
+            nc.sync.dma_start(
+                out=wlsc_t[32 * q : 32 * q + 4, :, :],
+                in_=wl_scales_i[:, 4 * q : 4 * q + 4, :].rearrange("a r n -> r a n"),
+            )
+
+        def load_wgo(lo, hi):
+            nc.sync.dma_start(out=wgo_t[:, lo:hi], in_=wgo[:, lo:hi])
 
         def gather_codes(g, lo, hi):
             nc.vector.tensor_copy(
                 out=v_codes[g][:, lo:hi], in_=tab_t[g][:].bitcast(U32).indirect(offs_t[:, lo // 16 : hi // 16])
             )
 
-        def quantise_wp(a, g, engine):
+        def gather_scales(lo, hi):
+            nc.vector.tensor_copy(
+                out=v_scales[:, lo:hi], in_=tabsc_t[:].bitcast(U8).indirect(offs_t[:, lo // 16 : hi // 16])
+            )
+
+        on_vector = nc.vector.tensor_copy
+        on_scalar = nc.scalar.copy
+
+        def quantise_wp(a, g, split):
             grouped = ring.tile([P, 4, P, 4], BF16, name="w_grouped", bufs=3, align_bytes=64)
             dst = grouped[:].rearrange("p t m j -> p m j t")
             src = wp_raw[a, g][:].rearrange("p j (m t) -> p m j t", t=4)
-            if engine == "H":
-                copy_on("V", dst[:, 0:80], src[:, 0:80])
-                copy_on("S", dst[:, 80:P], src[:, 80:P])
-            else:
-                copy_on(engine, dst, src)
+            if split > 0:
+                on_vector(out=dst[:, 0:split], in_=src[:, 0:split])
+            if split < P:
+                on_scalar(out=dst[:, split:P], in_=src[:, split:P])
             nc.vector.quantize_mx(
                 out=wp_codes[a, g][:].bitcast(FP8X4),
                 scales=wp_scales[a, g][:],
                 in_=grouped[:].rearrange("p t m j -> p (t m j)"),
             )
 
-        def quantise_wq(h, engine):
+        def quantise_wq(h, copy):
             grouped = ring.tile([P, RP, 256, 4], BF16, name="w_grouped", bufs=3, align_bytes=64)
             for a in range(RP):
-                copy_on(
-                    engine[a],
-                    grouped[:, a].rearrange("p (c i) j -> p c j i", i=4),
-                    wq_raw[h, a][:].rearrange("p j (c i) -> p c j i", i=4),
+                copy(
+                    out=grouped[:, a].rearrange("p (c i) j -> p c j i", i=4),
+                    in_=wq_raw[h, a][:].rearrange("p j (c i) -> p c j i", i=4),
                 )
             nc.vector.quantize_mx(
                 out=wq_codes[h][:].rearrange("p a n -> p (a n)").bitcast(FP8X4),
@@ -127,154 +136,123 @@ def tile_list_quadratic_state_prediction_kernel(
                 in_=grouped[:].rearrange("p a n j -> p (a n j)"),
             )
 
-        zq_codes = {}
-        zq_scales = {}
+        rows = {}
 
-        def z_pass(acc, a, t, g, lo, hi):
-            cols = slice(P * t, P * (t + 1))
-            nc.tensor.matmul_mx(
-                out=acc,
-                lhsT=wp_codes[a, g][:, cols].bitcast(FP8X4),
-                lhsT_scale=wp_scales[a, g][:, cols],
-                rhs=v_codes[g][:, lo:hi].bitcast(FP8X4),
-                rhs_scale=v_scales[4 * g : P, lo:hi],
-                start=(g == 0),
-                stop=(g == KP - 1),
-            )
-
-        bank_t = [psum.tile([P, 512], F32, name="bank%d" % u) for u in range(8)]
-
-        def make_zq(a, lo, hi, engines, which):
+        def make_rows(a, lo, hi, passes=(0, 1, 2)):
             width = hi - lo
-            banks = [bank_t[int(u)] for u in which]
-            spread = width == 256 and len(banks) == 4
-            if spread:
-                accs = [banks[t][:, 0:width] for t in range(4)]
-                for g in range(KP):
-                    for t in range(4):
-                        z_pass(accs[t], a, t, g, lo, hi)
-            else:
-                per_bank = 512 // width
-                accs = [banks[t // per_bank][:, width * (t % per_bank) : width * (t % per_bank + 1)] for t in range(4)]
-                for t in range(4):
-                    for g in range(KP):
-                        z_pass(accs[t], a, t, g, lo, hi)
-            rows = ring.tile([P, 2, 4, width], BF16, name="zq_rows", tag="stage", bufs=8, align_bytes=64)
-            for s, t in (
-                [(s, t) for s in range(2) for t in range(4)] if spread else [(s, t) for t in range(4) for s in range(2)]
-            ):
-                if s == 0:
-                    nc.scalar.activation(out=rows[:, s, t, :], in_=accs[t], func=ACT.Identity, bias=b_t[:, a, t : t + 1])
-                else:
-                    nc.scalar.activation(
-                        out=rows[:, s, t, :],
-                        in_=accs[t],
-                        func=ACT.Square,
-                        bias=rootb_t[:, a, t : t + 1],
-                        scale=root_t[:, a, t : t + 1],
-                    )
-            grouped = ring.tile([P, 2, width, 4], BF16, name="zq_grouped", tag="stage", bufs=8, align_bytes=64)
-            for s in range(2):
-                copy_on(
-                    engines[s],
-                    grouped[:, s].rearrange("p (c i) t -> p c t i", i=4),
-                    rows[:, s].rearrange("p t (c i) -> p c t i", i=4),
+            per_bank = 512 // width
+            accs = []
+            for u in range(4 // per_bank):
+                bank = psum.tile([P, per_bank, width], F32, name="z_bank", bufs=5)
+                for v in range(per_bank):
+                    cols = slice(P * len(accs), P * (len(accs) + 1))
+                    for g in passes:
+                        nc.tensor.matmul_mx(
+                            out=bank[:, v, :],
+                            lhsT=wp_codes[a, g][:, cols].bitcast(FP8X4),
+                            lhsT_scale=wp_scales[a, g][:, cols],
+                            rhs=v_codes[g][:, lo:hi].bitcast(FP8X4),
+                            rhs_scale=v_scales[4 * g : P, lo:hi],
+                            start=(g == passes[0]),
+                            stop=(g == passes[-1]),
+                        )
+                    accs.append(bank[:, v, :])
+            pair = [ring.tile([P, 4, width], BF16, name="zq_rows", bufs=6, align_bytes=64) for s in range(2)]
+            for t in range(4):
+                nc.scalar.activation(out=pair[0][:, t, :], in_=accs[t], func=ACT.Identity, bias=b_t[:, a, t : t + 1])
+                nc.scalar.activation(
+                    out=pair[1][:, t, :],
+                    in_=accs[t],
+                    func=ACT.Square,
+                    bias=rootb_t[:, a, t : t + 1],
+                    scale=root_t[:, a, t : t + 1],
                 )
+            for u in range(lo, hi, CHUNK):
+                for s in range(2):
+                    rows[s, a, u] = (pair[s], u - lo)
+
+        def quantise_rows(a, lo, hi, copies):
+            width = hi - lo
+            grouped = []
+            for s in range(2):
+                tile_s, first = rows[s, a, lo]
+                grouped.append(ring.tile([P, width, 4], BF16, name="zq_grouped", bufs=4, align_bytes=64))
+                copies[s](
+                    out=grouped[s][:].rearrange("p (c i) t -> p c t i", i=4),
+                    in_=tile_s[:, :, first : first + width].rearrange("p t (c i) -> p c t i", i=4),
+                )
+            for s in range(2):
                 nc.vector.quantize_mx(
                     out=zq_codes[s, a][:, lo:hi].bitcast(FP8X4),
                     scales=zq_scales[s, a][:, lo:hi],
-                    in_=grouped[:, s].rearrange("p n t -> p (n t)"),
+                    in_=grouped[s][:].rearrange("p n t -> p (n t)"),
                 )
 
-        for s in range(2):
-            for a in range(RP):
-                zq_codes[s, a] = keep.tile([P, S], U32, name="zq_codes%d%d" % (s, a), align_bytes=64)
-                zq_scales[s, a] = keep.tile([P, S], U8, name="zq_scales%d%d" % (s, a), align_bytes=64)
-
-        y_t = {}
-
-        def make_y(lo, hi, n, which):
-            width = hi - lo
+        def predict(lo, n, width=CHUNK):
+            hi = lo + width
             step = 512 if width == 512 else P
-            bank = bank_t[which]
+            bank = psum.tile([P, width], F32, name="y_bank", bufs=3)
             h, m = divmod(n, 2)
-            for u in range(0, width, step):
-                tok = slice(lo + u, lo + u + step)
-                for a in range(RP):
+            for a in range(RP):
+                nc.tensor.matmul_mx(
+                    out=bank[:],
+                    lhsT=wq_codes[h][:, a, P * m : P * (m + 1)].bitcast(FP8X4),
+                    lhsT_scale=wq_scales[h][:, a, P * m : P * (m + 1)],
+                    rhs=zq_codes[1, a][:, lo:hi].bitcast(FP8X4),
+                    rhs_scale=zq_scales[1, a][:, lo:hi],
+                    start=(a == 0),
+                    stop=False,
+                )
+                for u in range(0, width, step):
+                    tok = slice(lo + u, lo + u + step)
                     nc.tensor.matmul_mx(
                         out=bank[:, u : u + step],
                         lhsT=wl_t[:, a, 2 * P * n : 2 * P * (n + 1)].bitcast(FP4X4),
                         lhsT_scale=wlsc_t[:, a, :].bitcast(U8)[:, P * n : P * (n + 1)],
                         rhs=zq_codes[0, a][:, tok].bitcast(FP8X4),
                         rhs_scale=zq_scales[0, a][:, tok],
-                        start=(a == 0),
-                        stop=False,
-                    )
-                for a in range(RP):
-                    nc.tensor.matmul_mx(
-                        out=bank[:, u : u + step],
-                        lhsT=wq_codes[h][:, a, P * m : P * (m + 1)].bitcast(FP8X4),
-                        lhsT_scale=wq_scales[h][:, a, P * m : P * (m + 1)],
-                        rhs=zq_codes[1, a][:, tok].bitcast(FP8X4),
-                        rhs_scale=zq_scales[1, a][:, tok],
                         start=False,
-                        stop=(a == RP - 1),
+                        stop=(a == RP - 1 and u + step == width),
                     )
-            y_t[lo, n] = ring.tile([P, width], F32, name="y_t", bufs=6)
-            nc.scalar.activation(out=y_t[lo, n][:], in_=bank[:, 0:width], func=ACT.Identity, bias=c_t[:, n : n + 1])
-
-        def scatter(lo, hi, n):
+            y_t = ring.tile([P, width], F32, name="y_t", bufs=3)
+            nc.scalar.activation(out=y_t[:], in_=bank[:], func=ACT.Identity, bias=c_t[:, n : n + 1])
             nc.vector.tensor_tensor(
                 out=out_t[n][:].indirect(offs2_t[:, lo // 16 : hi // 16]),
-                in0=y_t[lo, n][:],
+                in0=y_t[:],
                 in1=wgo_t[:, lo:hi],
                 op=ALU.mult,
             )
 
-        nc.vector.memset(out_t[0][:], 0.0)
-        nc.vector.memset(out_t[1][:], 0.0)
-        nc.gpsimd.memset(out_t[2][:], 0.0)
-        nc.gpsimd.memset(out_t[3][:], 0.0)
+        def store(n):
+            nc.sync.dma_start(out=out[P * n : P * (n + 1), :], in_=out_t[n][:])
 
-        for step in LOADS.split():
-            if step == "offs":
-                nc.sync.dma_start(offs_t[:], offs)
-            elif step == "offs2":
-                nc.sync.dma_start(offs2_t[:], offs2)
-            elif step == "d":
-                nc.sync.dma_start(out=d_t[:], in_=d.rearrange("(a p t) -> p a t", a=RP, t=4))
-            elif step == "b":
-                nc.sync.dma_start(out=b_t[:], in_=b.rearrange("(a p t) -> p a t", a=RP, t=4))
-            elif step == "c":
-                with nc.allow_non_contiguous_dma(reason="one bias value a partition"):
-                    nc.sync.dma_start(out=c_t[:], in_=c.rearrange("(t p) -> p t", p=P))
-            elif step == "wl":
-                nc.sync.dma_start(out=wl_t[:].bitcast(I32), in_=wl_words.rearrange("a p n -> p a n").bitcast(I32))
-            elif step[0] == "T":
-                Q = int(step[1])
-                nc.sync.dma_start(out=tabsc_t[32 * Q : 32 * Q + 4 * KP, :], in_=tab_scales_i[:, 4 * Q : 4 * Q + 4, :])
-            elif step[0] == "A":
-                Q = int(step[1])
-                nc.sync.dma_start(out=tabsc_t[32 * Q : 32 * Q + 8, :], in_=tab_scales_i[0:2, 4 * Q : 4 * Q + 4, :])
-            elif step[0] == "B":
-                Q = int(step[1])
-                nc.sync.dma_start(out=tabsc_t[32 * Q + 8 : 32 * Q + 12, :], in_=tab_scales_i[2, 4 * Q : 4 * Q + 4, :])
-            elif step[0] == "L":
-                Q = int(step[1])
-                nc.sync.dma_start(
-                    out=wlsc_t[32 * Q : 32 * Q + 4, :, :],
-                    in_=wl_scales_i[:, 4 * Q : 4 * Q + 4, :].rearrange("a r n -> r a n"),
-                )
-            elif step[0] == "t":
-                load_tab(int(step[1]), int(step[2]))
-            elif step[0] == "p":
-                load_wp(int(step[1]), int(step[2]))
-            elif step[0] == "q":
-                load_wq(int(step[1]))
-            else:
-                h = int(step[1])
-                cols = slice(S // 2 * h, S // 2 * (h + 1))
-                nc.sync.dma_start(out=wgo_t[:, cols], in_=wgo[:, cols])
+        nc.vector.memset(tabsc_t[:], 0)
+        nc.vector.memset(wlsc_t[:], 0)
+
+        nc.sync.dma_start(offs_t[:], offs)
+        load_tab(0)
+        nc.scalar.dma_start(out=d_t[:], in_=d.rearrange("(a p t) -> p a t", a=RP, t=4))
+        nc.scalar.dma_start(out=b_t[:], in_=b.rearrange("(a p t) -> p a t", a=RP, t=4))
+        for q in range(4):
+            nc.scalar.dma_start(out=tabsc_t[32 * q : 32 * q + 4 * KP, :], in_=tab_scales_i[:, 4 * q : 4 * q + 4, :])
+        load_tab(1)
+        load_wp(0, 0)
+        load_tab(2)
+        load_wp(0, 1)
+        load_wp(0, 2)
+        load_wp(1, 0)
+        load_wp(1, 1)
+        load_wp(1, 2)
+        load_wq(0)
+        load_wq(1)
+        nc.sync.dma_start(out=wl_t[:].bitcast(I32), in_=wl_words.rearrange("a p n -> p a n").bitcast(I32))
+        for q in range(4):
+            load_wl_scales(q)
+        with nc.allow_non_contiguous_dma(reason="one bias value a partition"):
+            nc.sync.dma_start(out=c_t[:], in_=c.rearrange("(t p) -> p t", p=P))
+        nc.sync.dma_start(offs2_t[:], offs2)
+        load_wgo(0, 512)
+        load_wgo(512, S)
 
         root0_t = keep.tile([P, RP, 4], F32, name="root0_t")
         quot_t = keep.tile([P, RP, 4], F32, name="quot_t")
@@ -282,32 +260,57 @@ def tile_list_quadratic_state_prediction_kernel(
         rootb_t = keep.tile([P, RP, 4], F32, name="rootb_t")
         nc.scalar.activation(out=root0_t[:], in_=d_t[:], func=ACT.Sqrt)
         nc.vector.reciprocal(out=quot_t[:], in_=root0_t[:])
-        nc.vector.tensor_tensor(out=quot_t[:], in0=quot_t[:], in1=d_t[:], op=ALU.mult)
-        nc.vector.tensor_tensor(out=quot_t[:], in0=quot_t[:], in1=root0_t[:], op=ALU.add)
-        nc.vector.tensor_scalar(out=root_t[:], in0=quot_t[:], scalar1=0.5, scalar2=None, op0=ALU.mult)
-        nc.vector.tensor_tensor(out=rootb_t[:], in0=root_t[:], in1=b_t[:], op=ALU.mult)
+        nc.gpsimd.tensor_tensor(out=quot_t[:], in0=quot_t[:], in1=d_t[:], op=ALU.mult)
+        nc.gpsimd.tensor_tensor(out=quot_t[:], in0=quot_t[:], in1=root0_t[:], op=ALU.add)
+        nc.gpsimd.tensor_scalar(out=root_t[:], in0=quot_t[:], scalar1=0.5, scalar2=0.0, op0=ALU.mult, op1=ALU.add)
+        nc.gpsimd.tensor_tensor(out=rootb_t[:], in0=root_t[:], in1=b_t[:], op=ALU.mult)
 
-        for step in PLAN.split():
-            kind = step[0]
-            lo = 256 * int(step[1])
-            hi = 256 * int(step[2])
-            if kind == "g":
-                gather_codes(int(step[3]), lo, hi)
-            elif kind == "G":
-                nc.vector.tensor_copy(
-                    out=v_scales[:, lo:hi], in_=tabsc_t[:].bitcast(U8).indirect(offs_t[:, lo // 16 : hi // 16])
-                )
-            elif kind == "p":
-                quantise_wp(int(step[1]), int(step[2]), step[3])
-            elif kind == "z":
-                make_zq(int(step[3]), lo, hi, step[4:6], step[6:])
-            elif kind == "w":
-                quantise_wq(int(step[3]), step[4:6])
-            elif kind == "y":
-                make_y(lo, hi, int(step[3]), int(step[4]))
-            elif kind == "s":
-                for n in step[3:]:
-                    scatter(lo, hi, int(n))
-            else:
-                n = int(step[3])
-                nc.sync.dma_start(out=out[P * n : P * (n + 1), :], in_=out_t[n][:])
+        nc.vector.memset(out_t[0][:], 0.0)
+        nc.vector.memset(out_t[1][:], 0.0)
+        nc.gpsimd.memset(out_t[2][:], 0.0)
+        nc.gpsimd.memset(out_t[3][:], 0.0)
+        gather_codes(0, 0, S)
+        gather_codes(1, 0, S)
+        gather_scales(0, S)
+        quantise_wp(0, 0, 0)
+        gather_codes(2, 0, S)
+        quantise_wp(0, 1, 0)
+        quantise_wp(0, 2, 96)
+
+        make_rows(0, 0, 512)
+        quantise_wp(1, 0, P)
+        quantise_wp(1, 1, P)
+        quantise_wp(1, 2, P)
+        make_rows(1, 0, 256, (2, 0, 1))
+        quantise_rows(0, 0, 256, [on_vector, on_vector])
+        quantise_wq(0, on_vector)
+        quantise_rows(1, 0, 256, [on_vector, on_vector])
+        quantise_wq(1, on_scalar)
+        predict(0, 0)
+        predict(0, 1)
+        predict(0, 2)
+        quantise_rows(0, 256, 512, [on_vector, on_vector])
+        make_rows(1, 256, 512, (2, 0, 1))
+        quantise_rows(1, 256, 512, [on_scalar, on_scalar])
+        predict(0, 3)
+        make_rows(0, 512, S)
+        quantise_rows(0, 512, 768, [on_vector, on_vector])
+        make_rows(1, 512, 768, (2, 0, 1))
+        predict(256, 0)
+        quantise_rows(1, 512, 768, [on_scalar, on_scalar])
+        predict(256, 1)
+        predict(256, 2)
+        predict(256, 3)
+        make_rows(1, 768, S, (2, 0, 1))
+        quantise_rows(0, 768, S, [on_scalar, on_scalar])
+        predict(512, 0)
+        quantise_rows(1, 768, S, [on_scalar, on_scalar])
+        predict(512, 1)
+        predict(768, 0)
+        store(0)
+        predict(768, 1)
+        store(1)
+        predict(512, 2, 512)
+        store(2)
+        predict(512, 3, 512)
+        store(3)

@@ -157,7 +157,7 @@ def tile_list_quadratic_state_prediction_kernel(
                             stop=(g == passes[-1]),
                         )
                     accs.append(bank[:, v, :])
-            pair = [ring.tile([P, 4, width], BF16, name="zq_rows", bufs=6, align_bytes=64) for s in range(2)]
+            pair = [ring.tile([P, 4, width], BF16, name="zq_rows", bufs=5, align_bytes=64) for s in range(2)]
             for t in range(4):
                 nc.scalar.activation(out=pair[0][:, t, :], in_=accs[t], func=ACT.Identity, bias=b_t[:, a, t : t + 1])
                 nc.scalar.activation(
@@ -176,7 +176,7 @@ def tile_list_quadratic_state_prediction_kernel(
             grouped = []
             for s in range(2):
                 tile_s, first = rows[s, a, lo]
-                grouped.append(ring.tile([P, width, 4], BF16, name="zq_grouped", bufs=4, align_bytes=64))
+                grouped.append(ring.tile([P, width, 4], BF16, name="zq_grouped", bufs=3, align_bytes=64))
                 copies[s](
                     out=grouped[s][:].rearrange("p (c i) t -> p c t i", i=4),
                     in_=tile_s[:, :, first : first + width].rearrange("p t (c i) -> p c t i", i=4),
@@ -254,21 +254,10 @@ def tile_list_quadratic_state_prediction_kernel(
         load_wgo(0, 512)
         load_wgo(512, S)
 
-        root0_t = keep.tile([P, RP, 4], F32, name="root0_t")
-        quot_t = keep.tile([P, RP, 4], F32, name="quot_t")
-        root_t = keep.tile([P, RP, 4], F32, name="root_t")
-        rootb_t = keep.tile([P, RP, 4], F32, name="rootb_t")
-        nc.scalar.activation(out=root0_t[:], in_=d_t[:], func=ACT.Sqrt)
-        nc.vector.reciprocal(out=quot_t[:], in_=root0_t[:])
-        nc.gpsimd.tensor_tensor(out=quot_t[:], in0=quot_t[:], in1=d_t[:], op=ALU.mult)
-        nc.gpsimd.tensor_tensor(out=quot_t[:], in0=quot_t[:], in1=root0_t[:], op=ALU.add)
-        nc.gpsimd.tensor_scalar(out=root_t[:], in0=quot_t[:], scalar1=0.5, scalar2=0.0, op0=ALU.mult, op1=ALU.add)
-        nc.gpsimd.tensor_tensor(out=rootb_t[:], in0=root_t[:], in1=b_t[:], op=ALU.mult)
-
         nc.vector.memset(out_t[0][:], 0.0)
         nc.vector.memset(out_t[1][:], 0.0)
-        nc.gpsimd.memset(out_t[2][:], 0.0)
-        nc.gpsimd.memset(out_t[3][:], 0.0)
+        nc.vector.memset(out_t[2][:], 0.0)
+        nc.vector.memset(out_t[3][:], 0.0)
         gather_codes(0, 0, S)
         gather_codes(1, 0, S)
         gather_scales(0, S)
@@ -276,7 +265,16 @@ def tile_list_quadratic_state_prediction_kernel(
         gather_codes(2, 0, S)
         quantise_wp(0, 1, 0)
         quantise_wp(0, 2, 96)
-
+        root0_t = keep.tile([P, RP, 4], F32, name="root0_t")
+        quot_t = keep.tile([P, RP, 4], F32, name="quot_t")
+        root_t = keep.tile([P, RP, 4], F32, name="root_t")
+        rootb_t = keep.tile([P, RP, 4], F32, name="rootb_t")
+        nc.scalar.activation(out=root0_t[:], in_=d_t[:], func=ACT.Sqrt)
+        nc.vector.reciprocal(out=quot_t[:], in_=root0_t[:])
+        nc.vector.tensor_tensor(out=quot_t[:], in0=quot_t[:], in1=d_t[:], op=ALU.mult)
+        nc.vector.tensor_tensor(out=quot_t[:], in0=quot_t[:], in1=root0_t[:], op=ALU.add)
+        nc.vector.tensor_scalar(out=root_t[:], in0=quot_t[:], scalar1=0.5, scalar2=None, op0=ALU.mult)
+        nc.vector.tensor_tensor(out=rootb_t[:], in0=root_t[:], in1=b_t[:], op=ALU.mult)
         make_rows(0, 0, 512)
         quantise_wp(1, 0, P)
         quantise_wp(1, 1, P)
@@ -294,7 +292,7 @@ def tile_list_quadratic_state_prediction_kernel(
         quantise_rows(1, 256, 512, [on_scalar, on_scalar])
         predict(0, 3)
         make_rows(0, 512, S)
-        quantise_rows(0, 512, 768, [on_vector, on_vector])
+        quantise_rows(0, 512, S, [on_vector, on_vector])
         make_rows(1, 512, 768, (2, 0, 1))
         predict(256, 0)
         quantise_rows(1, 512, 768, [on_scalar, on_scalar])
@@ -302,7 +300,6 @@ def tile_list_quadratic_state_prediction_kernel(
         predict(256, 2)
         predict(256, 3)
         make_rows(1, 768, S, (2, 0, 1))
-        quantise_rows(0, 768, S, [on_scalar, on_scalar])
         predict(512, 0)
         quantise_rows(1, 768, S, [on_scalar, on_scalar])
         predict(512, 1)

@@ -138,7 +138,7 @@ def tile_list_quadratic_state_prediction_kernel(
 
         rows = {}
 
-        def make_rows(a, lo, hi, passes=(0, 1, 2)):
+        def make_rows(a, lo, hi, passes=(0, 1, 2), z_first=False):
             width = hi - lo
             per_bank = 512 // width
             accs = []
@@ -158,15 +158,18 @@ def tile_list_quadratic_state_prediction_kernel(
                         )
                     accs.append(bank[:, v, :])
             pair = [ring.tile([P, 4, width], BF16, name="zq_rows", bufs=5, align_bytes=64) for s in range(2)]
-            for t in range(4):
-                nc.scalar.activation(out=pair[0][:, t, :], in_=accs[t], func=ACT.Identity, bias=b_t[:, a, t : t + 1])
-                nc.scalar.activation(
-                    out=pair[1][:, t, :],
-                    in_=accs[t],
-                    func=ACT.Square,
-                    bias=rootb_t[:, a, t : t + 1],
-                    scale=root_t[:, a, t : t + 1],
-                )
+            reads = [(s, t) for s in range(2) for t in range(4)] if z_first else [(s, t) for t in range(4) for s in range(2)]
+            for s, t in reads:
+                if s == 0:
+                    nc.scalar.activation(out=pair[0][:, t, :], in_=accs[t], func=ACT.Identity, bias=b_t[:, a, t : t + 1])
+                else:
+                    nc.scalar.activation(
+                        out=pair[1][:, t, :],
+                        in_=accs[t],
+                        func=ACT.Square,
+                        bias=rootb_t[:, a, t : t + 1],
+                        scale=root_t[:, a, t : t + 1],
+                    )
             for u in range(lo, hi, CHUNK):
                 for s in range(2):
                     rows[s, a, u] = (pair[s], u - lo)
@@ -237,9 +240,9 @@ def tile_list_quadratic_state_prediction_kernel(
             nc.scalar.dma_start(out=tabsc_t[32 * q : 32 * q + 4 * KP, :], in_=tab_scales_i[:, 4 * q : 4 * q + 4, :])
         load_tab(1)
         load_wp(0, 0)
-        load_tab(2)
         load_wp(0, 1)
         load_wp(0, 2)
+        load_tab(2)
         load_wp(1, 0)
         load_wp(1, 1)
         load_wp(1, 2)
@@ -254,17 +257,16 @@ def tile_list_quadratic_state_prediction_kernel(
         load_wgo(0, 512)
         load_wgo(512, S)
 
-        nc.vector.memset(out_t[0][:], 0.0)
-        nc.vector.memset(out_t[1][:], 0.0)
-        nc.vector.memset(out_t[2][:], 0.0)
-        nc.vector.memset(out_t[3][:], 0.0)
+        for n in range(NT):
+            nc.vector.memset(out_t[n][:], 0.0)
         gather_codes(0, 0, S)
         gather_codes(1, 0, S)
         gather_scales(0, S)
         quantise_wp(0, 0, 0)
-        gather_codes(2, 0, S)
         quantise_wp(0, 1, 0)
-        quantise_wp(0, 2, 96)
+        quantise_wp(0, 2, P)
+        gather_codes(2, 0, 512)
+        gather_codes(2, 512, S)
         root0_t = keep.tile([P, RP, 4], F32, name="root0_t")
         quot_t = keep.tile([P, RP, 4], F32, name="quot_t")
         root_t = keep.tile([P, RP, 4], F32, name="root_t")
@@ -275,31 +277,32 @@ def tile_list_quadratic_state_prediction_kernel(
         nc.vector.tensor_tensor(out=quot_t[:], in0=quot_t[:], in1=root0_t[:], op=ALU.add)
         nc.vector.tensor_scalar(out=root_t[:], in0=quot_t[:], scalar1=0.5, scalar2=None, op0=ALU.mult)
         nc.vector.tensor_tensor(out=rootb_t[:], in0=root_t[:], in1=b_t[:], op=ALU.mult)
-        make_rows(0, 0, 512)
+        make_rows(0, 0, 512, z_first=True)
         quantise_wp(1, 0, P)
         quantise_wp(1, 1, P)
         quantise_wp(1, 2, P)
-        make_rows(1, 0, 256, (2, 0, 1))
+        make_rows(0, 512, S)
         quantise_rows(0, 0, 256, [on_vector, on_vector])
+        make_rows(1, 0, 256)
         quantise_wq(0, on_vector)
+        quantise_rows(0, 256, 512, [on_vector, on_vector])
         quantise_rows(1, 0, 256, [on_vector, on_vector])
         quantise_wq(1, on_scalar)
+        quantise_rows(0, 512, 768, [on_vector, on_vector])
         predict(0, 0)
         predict(0, 1)
-        predict(0, 2)
-        quantise_rows(0, 256, 512, [on_vector, on_vector])
-        make_rows(1, 256, 512, (2, 0, 1))
+        make_rows(1, 256, 512)
         quantise_rows(1, 256, 512, [on_scalar, on_scalar])
+        predict(0, 2)
         predict(0, 3)
-        make_rows(0, 512, S)
-        quantise_rows(0, 512, S, [on_vector, on_vector])
-        make_rows(1, 512, 768, (2, 0, 1))
+        make_rows(1, 512, 768)
         predict(256, 0)
-        quantise_rows(1, 512, 768, [on_scalar, on_scalar])
         predict(256, 1)
+        quantise_rows(1, 512, 768, [on_scalar, on_scalar])
         predict(256, 2)
+        quantise_rows(0, 768, S, [on_scalar, on_vector])
         predict(256, 3)
-        make_rows(1, 768, S, (2, 0, 1))
+        make_rows(1, 768, S)
         predict(512, 0)
         quantise_rows(1, 768, S, [on_scalar, on_scalar])
         predict(512, 1)

@@ -157,7 +157,7 @@ def tile_list_quadratic_state_prediction_kernel(
                             stop=(g == passes[-1]),
                         )
                     accs.append(bank[:, v, :])
-            pair = [ring.tile([P, 4, width], BF16, name="zq_rows", bufs=5, align_bytes=64) for s in range(2)]
+            pair = [ring.tile([P, 4, width], BF16, name="zq_rows", bufs=6, align_bytes=64) for s in range(2)]
             reads = [(s, t) for s in range(2) for t in range(4)] if z_first else [(s, t) for t in range(4) for s in range(2)]
             for s, t in reads:
                 if s == 0:
@@ -179,7 +179,7 @@ def tile_list_quadratic_state_prediction_kernel(
             grouped = []
             for s in range(2):
                 tile_s, first = rows[s, a, lo]
-                grouped.append(ring.tile([P, width, 4], BF16, name="zq_grouped", bufs=3, align_bytes=64))
+                grouped.append(ring.tile([P, width, 4], BF16, name="zq_grouped", bufs=4, align_bytes=64))
                 copies[s](
                     out=grouped[s][:].rearrange("p (c i) t -> p c t i", i=4),
                     in_=tile_s[:, :, first : first + width].rearrange("p t (c i) -> p c t i", i=4),
@@ -217,7 +217,7 @@ def tile_list_quadratic_state_prediction_kernel(
                         start=False,
                         stop=(a == RP - 1 and u + step == width),
                     )
-            y_t = ring.tile([P, width], F32, name="y_t", bufs=3)
+            y_t = ring.tile([P, width], F32, name="y_t", bufs=4)
             nc.scalar.activation(out=y_t[:], in_=bank[:], func=ACT.Identity, bias=c_t[:, n : n + 1])
             nc.vector.tensor_tensor(
                 out=out_t[n][:].indirect(offs2_t[:, lo // 16 : hi // 16]),
@@ -232,8 +232,8 @@ def tile_list_quadratic_state_prediction_kernel(
         nc.vector.memset(tabsc_t[:], 0)
         nc.vector.memset(wlsc_t[:], 0)
 
-        nc.sync.dma_start(offs_t[:], offs)
         load_tab(0)
+        nc.sync.dma_start(offs_t[:], offs)
         nc.scalar.dma_start(out=d_t[:], in_=d.rearrange("(a p t) -> p a t", a=RP, t=4))
         nc.scalar.dma_start(out=b_t[:], in_=b.rearrange("(a p t) -> p a t", a=RP, t=4))
         for q in range(4):
@@ -300,17 +300,18 @@ def tile_list_quadratic_state_prediction_kernel(
         predict(256, 1)
         quantise_rows(1, 512, 768, [on_scalar, on_scalar])
         predict(256, 2)
-        quantise_rows(0, 768, S, [on_scalar, on_vector])
+        quantise_rows(0, 768, S, [on_scalar, on_scalar])
         predict(256, 3)
-        make_rows(1, 768, S)
         predict(512, 0)
-        quantise_rows(1, 768, S, [on_scalar, on_scalar])
+        make_rows(1, 768, S)
         predict(512, 1)
+        quantise_rows(1, 768, S, [on_scalar, on_scalar])
+        predict(512, 2)
         predict(768, 0)
         store(0)
         predict(768, 1)
         store(1)
-        predict(512, 2, 512)
+        predict(768, 2)
         store(2)
         predict(512, 3, 512)
         store(3)

@@ -110,7 +110,7 @@ def tile_list_quadratic_state_prediction_kernel(
         on_scalar = nc.scalar.copy
 
         def quantise_wp(a, g, split):
-            grouped = ring.tile([P, 4, P, 4], BF16, name="w_grouped", bufs=3, align_bytes=64)
+            grouped = ring.tile([P, 4, P, 4], BF16, name="grouped", bufs=5, align_bytes=64)
             dst = grouped[:].rearrange("p t m j -> p m j t")
             src = wp_raw[a, g][:].rearrange("p j (m t) -> p m j t", t=4)
             if split > 0:
@@ -124,7 +124,7 @@ def tile_list_quadratic_state_prediction_kernel(
             )
 
         def quantise_wq(h, copy):
-            grouped = ring.tile([P, RP, 256, 4], BF16, name="w_grouped", bufs=3, align_bytes=64)
+            grouped = ring.tile([P, RP, 256, 4], BF16, name="grouped", bufs=5, align_bytes=64)
             for a in range(RP):
                 copy(
                     out=grouped[:, a].rearrange("p (c i) j -> p c j i", i=4),
@@ -174,17 +174,17 @@ def tile_list_quadratic_state_prediction_kernel(
                 for s in range(2):
                     rows[s, a, u] = (pair[s], u - lo)
 
-        def quantise_rows(a, lo, hi, copies):
+        def quantise_rows(a, lo, hi, copies, which=(0, 1)):
             width = hi - lo
-            grouped = []
-            for s in range(2):
+            grouped = {}
+            for s in which:
                 tile_s, first = rows[s, a, lo]
-                grouped.append(ring.tile([P, width, 4], BF16, name="zq_grouped", bufs=4, align_bytes=64))
+                grouped[s] = ring.tile([P, width, 4], BF16, name="grouped", bufs=5, align_bytes=64)
                 copies[s](
                     out=grouped[s][:].rearrange("p (c i) t -> p c t i", i=4),
                     in_=tile_s[:, :, first : first + width].rearrange("p t (c i) -> p c t i", i=4),
                 )
-            for s in range(2):
+            for s in which:
                 nc.vector.quantize_mx(
                     out=zq_codes[s, a][:, lo:hi].bitcast(FP8X4),
                     scales=zq_scales[s, a][:, lo:hi],
@@ -263,8 +263,8 @@ def tile_list_quadratic_state_prediction_kernel(
         gather_codes(1, 0, S)
         gather_scales(0, S)
         quantise_wp(0, 0, 0)
-        quantise_wp(0, 1, 0)
-        quantise_wp(0, 2, P)
+        quantise_wp(0, 1, 32)
+        quantise_wp(0, 2, 64)
         gather_codes(2, 0, 512)
         gather_codes(2, 512, S)
         root0_t = keep.tile([P, RP, 4], F32, name="root0_t")
@@ -280,10 +280,11 @@ def tile_list_quadratic_state_prediction_kernel(
         make_rows(0, 0, 512, z_first=True)
         quantise_wp(1, 0, P)
         quantise_wp(1, 1, P)
+        quantise_rows(0, 0, 256, [on_vector, on_vector], (0,))
         quantise_wp(1, 2, P)
         make_rows(0, 512, S)
-        quantise_rows(0, 0, 256, [on_vector, on_vector])
-        make_rows(1, 0, 256)
+        quantise_rows(0, 0, 256, [on_vector, on_vector], (1,))
+        make_rows(1, 0, 256, (2, 0, 1))
         quantise_wq(0, on_vector)
         quantise_rows(0, 256, 512, [on_vector, on_vector])
         quantise_rows(1, 0, 256, [on_vector, on_vector])

@@ -138,9 +138,9 @@ def tile_list_quadratic_state_prediction_kernel(
 
         rows = {}
 
-        def make_rows(a, lo, hi, passes=(0, 1, 2), z_first=False):
+        def make_rows(a, lo, hi, passes=(0, 1, 2), z_first=False, spread=False):
             width = hi - lo
-            per_bank = 512 // width
+            per_bank = 1 if spread else 512 // width
             accs = []
             for u in range(4 // per_bank):
                 bank = psum.tile([P, per_bank, width], F32, name="z_bank", bufs=5)
@@ -265,7 +265,8 @@ def tile_list_quadratic_state_prediction_kernel(
         quantise_wp(0, 0, 0)
         quantise_wp(0, 1, 32)
         quantise_wp(0, 2, 64)
-        gather_codes(2, 0, 512)
+        gather_codes(2, 0, 256)
+        gather_codes(2, 256, 512)
         gather_codes(2, 512, S)
         root0_t = keep.tile([P, RP, 4], F32, name="root0_t")
         quot_t = keep.tile([P, RP, 4], F32, name="quot_t")
@@ -277,22 +278,25 @@ def tile_list_quadratic_state_prediction_kernel(
         nc.vector.tensor_tensor(out=quot_t[:], in0=quot_t[:], in1=root0_t[:], op=ALU.add)
         nc.vector.tensor_scalar(out=root_t[:], in0=quot_t[:], scalar1=0.5, scalar2=None, op0=ALU.mult)
         nc.vector.tensor_tensor(out=rootb_t[:], in0=root_t[:], in1=b_t[:], op=ALU.mult)
-        make_rows(0, 0, 512, z_first=True)
+        make_rows(0, 0, 256, z_first=True, spread=True)
+        make_rows(0, 256, 512)
         quantise_wp(1, 0, P)
-        quantise_wp(1, 1, P)
         quantise_rows(0, 0, 256, [on_vector, on_vector], (0,))
+        quantise_wp(1, 1, P)
+        quantise_rows(0, 0, 256, [on_vector, on_vector], (1,))
         quantise_wp(1, 2, P)
         make_rows(0, 512, S)
-        quantise_rows(0, 0, 256, [on_vector, on_vector], (1,))
-        make_rows(1, 0, 256, (2, 0, 1))
+        quantise_rows(0, 256, 512, [on_vector, on_vector], (0,))
+        make_rows(1, 0, 256, spread=True)
         quantise_wq(0, on_vector)
-        quantise_rows(0, 256, 512, [on_vector, on_vector])
+        quantise_rows(0, 256, 512, [on_vector, on_vector], (1,))
+        quantise_rows(0, 512, 768, [on_vector, on_vector], (0,))
         quantise_rows(1, 0, 256, [on_vector, on_vector])
         quantise_wq(1, on_scalar)
-        quantise_rows(0, 512, 768, [on_vector, on_vector])
+        quantise_rows(0, 512, 768, [on_vector, on_vector], (1,))
         predict(0, 0)
         predict(0, 1)
-        make_rows(1, 256, 512)
+        make_rows(1, 256, 512, (2, 0, 1))
         quantise_rows(1, 256, 512, [on_scalar, on_scalar])
         predict(0, 2)
         predict(0, 3)

@@ -55,10 +55,7 @@ def tile_list_quadratic_state_prediction_kernel(
                 wp_raw[a, g] = keep.tile([P, 4, 512], F32, name="wp_raw%d%d" % (a, g))
                 wp_codes[a, g] = keep.tile([P, 512], U32, name="wp_codes%d%d" % (a, g), align_bytes=64)
                 wp_scales[a, g] = keep.tile([P, 512], U8, name="wp_scales%d%d" % (a, g), align_bytes=64)
-        wq_raw = {}
-        for h in range(2):
-            for a in range(RP):
-                wq_raw[h, a] = keep.tile([P, 4, 256], F32, name="wq_raw%d%d" % (h, a))
+        wq_raw = [keep.tile([P, 4, N], F32, name="wq_raw%d" % a) for a in range(RP)]
         wq_codes = [keep.tile([P, RP, 256], U32, name="wq_codes%d" % h, align_bytes=64) for h in range(2)]
         wq_scales = [keep.tile([P, RP, 256], U8, name="wq_scales%d" % h, align_bytes=64) for h in range(2)]
         zq_codes = {}
@@ -80,12 +77,8 @@ def tile_list_quadratic_state_prediction_kernel(
                 in_=wp[512 * g : 512 * (g + 1), 512 * a : 512 * (a + 1)].rearrange("(p j) c -> p j c", j=4),
             )
 
-        def load_wq(h):
-            for a in range(RP):
-                nc.sync.dma_start(
-                    out=wq_raw[h, a][:],
-                    in_=wq[512 * a : 512 * (a + 1), 256 * h : 256 * (h + 1)].rearrange("(p j) c -> p j c", j=4),
-                )
+        def load_wq(a):
+            nc.sync.dma_start(out=wq_raw[a][:], in_=wq[512 * a : 512 * (a + 1), :].rearrange("(p j) c -> p j c", j=4))
 
         def load_wl_scales(q):
             nc.sync.dma_start(
@@ -128,7 +121,7 @@ def tile_list_quadratic_state_prediction_kernel(
             for a in range(RP):
                 copy(
                     out=grouped[:, a].rearrange("p (c i) j -> p c j i", i=4),
-                    in_=wq_raw[h, a][:].rearrange("p j (c i) -> p c j i", i=4),
+                    in_=wq_raw[a][:, :, 256 * h : 256 * (h + 1)].rearrange("p j (c i) -> p c j i", i=4),
                 )
             nc.vector.quantize_mx(
                 out=wq_codes[h][:].rearrange("p a n -> p (a n)").bitcast(FP8X4),

@@ -300,16 +300,15 @@ def tile_list_quadratic_state_prediction_kernel(
         predict(256, 2)
         quantise_rows(0, 768, S, [on_scalar, on_scalar])
         predict(256, 3)
-        predict(512, 0)
         make_rows(1, 768, S)
-        predict(512, 1)
+        predict(512, 0)
         quantise_rows(1, 768, S, [on_scalar, on_scalar])
-        predict(512, 2)
+        predict(512, 1)
         predict(768, 0)
         store(0)
         predict(768, 1)
         store(1)
-        predict(768, 2)
+        predict(512, 2, 512)
         store(2)
         predict(512, 3, 512)
         store(3)

@@ -210,14 +210,11 @@ def tile_list_quadratic_state_prediction_kernel(
                         start=False,
                         stop=(a == RP - 1 and u + step == width),
                     )
-            y_t = ring.tile([P, width], F32, name="y_t", bufs=4)
+            y_t = ring.tile([P, width], F32, name="y_t", bufs=2)
             nc.scalar.activation(out=y_t[:], in_=bank[:], func=ACT.Identity, bias=c_t[:, n : n + 1])
-            nc.vector.tensor_tensor(
-                out=out_t[n][:].indirect(offs2_t[:, lo // 16 : hi // 16]),
-                in0=y_t[:],
-                in1=wgo_t[:, lo:hi],
-                op=ALU.mult,
-            )
+            yw_t = ring.tile([P, width], F32, name="yw_t", bufs=3)
+            nc.gpsimd.tensor_tensor(out=yw_t[:], in0=y_t[:], in1=wgo_t[:, lo:hi], op=ALU.mult)
+            nc.vector.tensor_copy(out=out_t[n][:].indirect(offs2_t[:, lo // 16 : hi // 16]), in_=yw_t[:])
 
         def store(n):
             nc.sync.dma_start(out=out[P * n : P * (n + 1), :], in_=out_t[n][:])

@@ -36,7 +36,6 @@ def tile_list_quadratic_state_prediction_kernel(
         offs_t = lists.tile([P, S // 16], U16, name="offs_t")
         offs2_t = lists.tile([P, S // 16], U16, name="offs2_t")
 
-        tab_t = [keep.tile([P, T], I32, name="tab_t%d" % g, align_bytes=64) for g in range(KP)]
         tabsc_t = keep.tile([P, T // 4], I32, name="tabsc_t", align_bytes=64)
         v_codes = [keep.tile([P, S], U32, name="v_codes%d" % g, align_bytes=64) for g in range(KP)]
         v_scales = keep.tile([P, S], U8, name="v_scales", align_bytes=64)
@@ -47,37 +46,34 @@ def tile_list_quadratic_state_prediction_kernel(
         c_t = keep.tile([P, NT], F32, name="c_t")
         wgo_t = keep.tile([P, S], F32, name="wgo_t")
         out_t = [keep.tile([P, T2], F32, name="out_t%d" % n) for n in range(NT)]
+        tab_t = {}
         wp_raw = {}
+        wq_raw = {}
         wp_codes = {}
         wp_scales = {}
-        for a in range(RP):
-            for g in range(KP):
-                wp_raw[a, g] = keep.tile([P, 4, 512], F32, name="wp_raw%d%d" % (a, g))
-                wp_codes[a, g] = keep.tile([P, 512], U32, name="wp_codes%d%d" % (a, g), align_bytes=64)
-                wp_scales[a, g] = keep.tile([P, 512], U8, name="wp_scales%d%d" % (a, g), align_bytes=64)
-        wq_raw = [keep.tile([P, 4, N], F32, name="wq_raw%d" % a) for a in range(RP)]
-        wq_codes = [keep.tile([P, RP, 256], U32, name="wq_codes%d" % h, align_bytes=64) for h in range(2)]
-        wq_scales = [keep.tile([P, RP, 256], U8, name="wq_scales%d" % h, align_bytes=64) for h in range(2)]
+        wq_codes = {}
+        wq_scales = {}
         zq_codes = {}
         zq_scales = {}
-        for s in range(2):
-            for a in range(RP):
-                zq_codes[s, a] = keep.tile([P, S], U32, name="zq_codes%d%d" % (s, a), align_bytes=64)
-                zq_scales[s, a] = keep.tile([P, S], U8, name="zq_scales%d%d" % (s, a), align_bytes=64)
+        rows = {}
+        stage = {}
 
         tab_scales_i = tab_scales.bitcast(I32)
         wl_scales_i = wl_scales.bitcast(I32)
 
         def load_tab(g):
+            tab_t[g] = ring.tile([P, T], I32, name="raw", bufs=6, align_bytes=64)
             nc.sync.dma_start(out=tab_t[g][:], in_=tab_words[g].rearrange("p t i -> p (t i)").bitcast(I32))
 
         def load_wp(a, g):
+            wp_raw[a, g] = ring.tile([P, 4, 512], F32, name="raw", bufs=6, align_bytes=64)
             nc.sync.dma_start(
                 out=wp_raw[a, g][:],
                 in_=wp[512 * g : 512 * (g + 1), 512 * a : 512 * (a + 1)].rearrange("(p j) c -> p j c", j=4),
             )
 
         def load_wq(a):
+            wq_raw[a] = ring.tile([P, 4, N], F32, name="raw", bufs=6, align_bytes=64)
             nc.sync.dma_start(out=wq_raw[a][:], in_=wq[512 * a : 512 * (a + 1), :].rearrange("(p j) c -> p j c", j=4))
 
         def load_wl_scales(q):
@@ -102,119 +98,210 @@ def tile_list_quadratic_state_prediction_kernel(
         on_vector = nc.vector.tensor_copy
         on_scalar = nc.scalar.copy
 
-        def quantise_wp(a, g, split):
-            grouped = ring.tile([P, 4, P, 4], BF16, name="grouped", bufs=5, align_bytes=64)
+        def grouped_tile(shape):
+            return ring.tile(shape, BF16, name="grouped", bufs=9, align_bytes=64)
+
+        def quantise(codes, scales, src):
+            nc.vector.quantize_mx(out=codes.bitcast(FP8X4), scales=scales, in_=src)
+
+        def cast_wp(a, g, split):
+            grouped = grouped_tile([P, 4, P, 4])
             dst = grouped[:].rearrange("p t m j -> p m j t")
             src = wp_raw[a, g][:].rearrange("p j (m t) -> p m j t", t=4)
             if split > 0:
                 on_vector(out=dst[:, 0:split], in_=src[:, 0:split])
             if split < P:
                 on_scalar(out=dst[:, split:P], in_=src[:, split:P])
-            nc.vector.quantize_mx(
-                out=wp_codes[a, g][:].bitcast(FP8X4),
-                scales=wp_scales[a, g][:],
-                in_=grouped[:].rearrange("p t m j -> p (t m j)"),
+            stage["wp", a, g] = grouped
+
+        def quantise_wp(a, g, parts=1):
+            wp_codes[a, g] = keep.tile([P, 512], U32, name="wp_codes%d%d" % (a, g), align_bytes=64)
+            wp_scales[a, g] = ring.tile([P, 512], U8, name="early_scales", bufs=14, align_bytes=64)
+            flat = stage["wp", a, g][:].rearrange("p t m j -> p (t m j)")
+            step = 512 // parts
+            for u in range(0, 512, step):
+                quantise(wp_codes[a, g][:, u : u + step], wp_scales[a, g][:, u : u + step], flat[:, 4 * u : 4 * (u + step)])
+
+        def cast_wq(h, a, copy, dst):
+            copy(
+                out=dst.rearrange("p (c i) j -> p c j i", i=4),
+                in_=wq_raw[a][:, :, 256 * h : 256 * (h + 1)].rearrange("p j (c i) -> p c j i", i=4),
             )
 
-        def quantise_wq(h, copy):
-            grouped = ring.tile([P, RP, 256, 4], BF16, name="grouped", bufs=5, align_bytes=64)
-            for a in range(RP):
-                copy(
-                    out=grouped[:, a].rearrange("p (c i) j -> p c j i", i=4),
-                    in_=wq_raw[a][:, :, 256 * h : 256 * (h + 1)].rearrange("p j (c i) -> p c j i", i=4),
-                )
-            nc.vector.quantize_mx(
-                out=wq_codes[h][:].rearrange("p a n -> p (a n)").bitcast(FP8X4),
-                scales=wq_scales[h][:].rearrange("p a n -> p (a n)"),
-                in_=grouped[:].rearrange("p a n j -> p (a n j)"),
+        def quantise_wq(h, halves, grouped, tag):
+            codes = keep.tile([P, len(halves), 256], U32, name="wq_codes%d_%d" % (h, halves[0]), align_bytes=64)
+            scales = ring.tile([P, len(halves), 256], U8, name=tag, bufs=14, align_bytes=64)
+            quantise(
+                codes[:].rearrange("p a n -> p (a n)"),
+                scales[:].rearrange("p a n -> p (a n)"),
+                grouped[:].rearrange("p a n j -> p (a n j)"),
             )
+            for i, a in enumerate(halves):
+                for m in range(2):
+                    wq_codes[a, 2 * h + m] = codes[:, i, P * m : P * (m + 1)]
+                    wq_scales[a, 2 * h + m] = scales[:, i, P * m : P * (m + 1)]
 
-        rows = {}
-
-        def make_rows(a, lo, hi, passes=(0, 1, 2), z_first=False, spread=False):
-            width = hi - lo
-            per_bank = 1 if spread else 512 // width
-            accs = []
-            for u in range(4 // per_bank):
-                bank = psum.tile([P, per_bank, width], F32, name="z_bank", bufs=5)
-                for v in range(per_bank):
-                    cols = slice(P * len(accs), P * (len(accs) + 1))
-                    for g in passes:
+        def multiply_rows(a, lo, ts, spread=False):
+            groups = [[t] for t in ts] if spread else [list(ts)]
+            accs = {}
+            for group in groups:
+                bank = psum.tile([P, len(group), CHUNK], F32, name="bank", bufs=8)
+                for v, t in enumerate(group):
+                    cols = slice(P * t, P * (t + 1))
+                    for g in range(KP):
                         nc.tensor.matmul_mx(
                             out=bank[:, v, :],
                             lhsT=wp_codes[a, g][:, cols].bitcast(FP8X4),
                             lhsT_scale=wp_scales[a, g][:, cols],
-                            rhs=v_codes[g][:, lo:hi].bitcast(FP8X4),
-                            rhs_scale=v_scales[4 * g : P, lo:hi],
-                            start=(g == passes[0]),
-                            stop=(g == passes[-1]),
+                            rhs=v_codes[g][:, lo : lo + CHUNK].bitcast(FP8X4),
+                            rhs_scale=v_scales[4 * g : P, lo : lo + CHUNK],
+                            start=(g == 0),
+                            stop=(g == KP - 1),
                         )
-                    accs.append(bank[:, v, :])
-            pair = [ring.tile([P, 4, width], BF16, name="zq_rows", bufs=6, align_bytes=64) for s in range(2)]
-            reads = [(s, t) for s in range(2) for t in range(4)] if z_first else [(s, t) for t in range(4) for s in range(2)]
-            for s, t in reads:
-                if s == 0:
-                    nc.scalar.activation(out=pair[0][:, t, :], in_=accs[t], func=ACT.Identity, bias=b_t[:, a, t : t + 1])
+                    accs[t] = bank[:, v, :]
+            return accs
+
+        def read_rows(a, lo, accs, which=(0, 1), staged=(), behind_y=False):
+            for s in which:
+                if (s, a, lo) in rows:
+                    continue
+                if behind_y and s == 0:
+                    rows[s, a, lo] = ring.tile([P, 4, CHUNK], BF16, name="y_t", bufs=4, align_bytes=64)
+                elif s in staged:
+                    rows[s, a, lo] = grouped_tile([P, 4, CHUNK])
                 else:
-                    nc.scalar.activation(
-                        out=pair[1][:, t, :],
-                        in_=accs[t],
-                        func=ACT.Square,
-                        bias=rootb_t[:, a, t : t + 1],
-                        scale=root_t[:, a, t : t + 1],
-                    )
-            for u in range(lo, hi, CHUNK):
-                for s in range(2):
-                    rows[s, a, u] = (pair[s], u - lo)
-
-        def quantise_rows(a, lo, hi, copies, which=(0, 1)):
-            width = hi - lo
-            grouped = {}
+                    rows[s, a, lo] = ring.tile([P, 4, CHUNK], BF16, name="zq_rows", bufs=10, align_bytes=64)
             for s in which:
-                tile_s, first = rows[s, a, lo]
-                grouped[s] = ring.tile([P, width, 4], BF16, name="grouped", bufs=5, align_bytes=64)
-                copies[s](
-                    out=grouped[s][:].rearrange("p (c i) t -> p c t i", i=4),
-                    in_=tile_s[:, :, first : first + width].rearrange("p t (c i) -> p c t i", i=4),
-                )
-            for s in which:
-                nc.vector.quantize_mx(
-                    out=zq_codes[s, a][:, lo:hi].bitcast(FP8X4),
-                    scales=zq_scales[s, a][:, lo:hi],
-                    in_=grouped[s][:].rearrange("p n t -> p (n t)"),
-                )
+                for t in sorted(accs):
+                    if s == 0:
+                        nc.scalar.activation(
+                            out=rows[0, a, lo][:, t, :], in_=accs[t], func=ACT.Identity, bias=b_t[:, a, t : t + 1]
+                        )
+                    else:
+                        nc.scalar.activation(
+                            out=rows[1, a, lo][:, t, :],
+                            in_=accs[t],
+                            func=ACT.Square,
+                            bias=rootb_t[:, a, t : t + 1],
+                            scale=root_t[:, a, t : t + 1],
+                        )
 
-        def predict(lo, n, width=CHUNK):
-            hi = lo + width
-            step = 512 if width == 512 else P
-            bank = psum.tile([P, width], F32, name="y_bank", bufs=3)
-            h, m = divmod(n, 2)
-            for a in range(RP):
-                nc.tensor.matmul_mx(
-                    out=bank[:],
-                    lhsT=wq_codes[h][:, a, P * m : P * (m + 1)].bitcast(FP8X4),
-                    lhsT_scale=wq_scales[h][:, a, P * m : P * (m + 1)],
-                    rhs=zq_codes[1, a][:, lo:hi].bitcast(FP8X4),
-                    rhs_scale=zq_scales[1, a][:, lo:hi],
-                    start=(a == 0),
-                    stop=False,
-                )
-                for u in range(0, width, step):
-                    tok = slice(lo + u, lo + u + step)
+        def make_rows(a, lo, ts, spread=False):
+            read_rows(a, lo, multiply_rows(a, lo, ts, spread))
+
+        def weave(s, a, lo, copy, dst):
+            copy(
+                out=dst.rearrange("p (c i) t -> p c t i", i=4),
+                in_=rows[s, a, lo][:].rearrange("p t (c i) -> p c t i", i=4),
+            )
+
+        def weave_on_gpsimd(s, a, lo, dst):
+            nc.gpsimd.tensor_scalar(
+                out=dst, in0=rows[s, a, lo][:].rearrange("p t n -> p n t"), scalar1=1.0, scalar2=0.0, op0=ALU.mult, op1=ALU.add
+            )
+
+        def first_weave(s, a, lo=0):
+            stage["zq", s, a, lo] = grouped_tile([P, CHUNK, 4])
+            weave(s, a, lo, on_vector, stage["zq", s, a, lo][:])
+
+        def quantise_one(s, a, lo, early=False):
+            codes = keep.tile([P, CHUNK], U32, name="codes%d%d_%d" % (s, a, lo), align_bytes=64)
+            tag = "early_scales" if lo == 0 or early else "held"
+            scales = ring.tile([P, CHUNK], U8, name=tag, bufs=14, align_bytes=64)
+            quantise(codes[:], scales[:], stage["zq", s, a, lo][:].rearrange("p n t -> p (n t)"))
+            zq_codes[s, a, lo] = codes[:]
+            zq_scales[s, a, lo] = scales[:]
+
+        def weave_on_scalar(s, a, lo, dst):
+            weave(s, a, lo, on_scalar, dst)
+
+        def weave_pair(a, lo):
+            grouped = grouped_tile([P, 2, CHUNK, 4])
+            for s in range(2):
+                weave_on_scalar(s, a, lo, grouped[:, s])
+            stage["pair", a, lo] = grouped
+
+        def weave_beside(s, a, lo, previous=None):
+            if previous is None:
+                lone = ring.tile([P, CHUNK, 4], BF16, name="pool_out", bufs=6, align_bytes=64)
+            else:
+                lone = stage["zq", s, a, previous]
+            weave_on_gpsimd(s, a, lo, lone[:])
+            stage["zq", s, a, lo] = lone
+
+        def quantise_pair(a, lo):
+            codes = keep.tile([P, 2, CHUNK], U32, name="pair_codes%d_%d" % (a, lo), align_bytes=64)
+            scales = ring.tile([P, 2, CHUNK], U8, name="held", bufs=14, align_bytes=64)
+            quantise(
+                codes[:].rearrange("p s n -> p (s n)"),
+                scales[:].rearrange("p s n -> p (s n)"),
+                stage["pair", a, lo][:].rearrange("p s n t -> p (s n t)"),
+            )
+            for s in range(2):
+                zq_codes[s, a, lo] = codes[:, s, :]
+                zq_scales[s, a, lo] = scales[:, s, :]
+
+        def products(lo, n, width=CHUNK, ahead=False):
+            bank = psum.tile([P, width], F32, name="bank", bufs=8)
+            for first in range(0, width, CHUNK):
+                wq_passes = [("wq", a, 0, CHUNK) for a in range(RP)]
+                wl_passes = [("wl", a, u, P) for a in range(RP) for u in range(0, CHUNK, P)]
+                if ahead:
+                    passes = wq_passes[:1] + wl_passes + wq_passes[1:]
+                else:
+                    passes = wl_passes + (wq_passes if lo == 0 else wq_passes[::-1])
+                for i, (kind, a, u, count) in enumerate(passes):
+                    if kind == "wq":
+                        weights = wq_codes[a, n].bitcast(FP8X4)
+                        weight_scales = wq_scales[a, n]
+                    else:
+                        weights = wl_t[:, a, 2 * P * n : 2 * P * (n + 1)].bitcast(FP4X4)
+                        weight_scales = wlsc_t[:, a, :].bitcast(U8)[:, P * n : P * (n + 1)]
+                    s = 1 if kind == "wq" else 0
                     nc.tensor.matmul_mx(
-                        out=bank[:, u : u + step],
-                        lhsT=wl_t[:, a, 2 * P * n : 2 * P * (n + 1)].bitcast(FP4X4),
-                        lhsT_scale=wlsc_t[:, a, :].bitcast(U8)[:, P * n : P * (n + 1)],
-                        rhs=zq_codes[0, a][:, tok].bitcast(FP8X4),
-                        rhs_scale=zq_scales[0, a][:, tok],
-                        start=False,
-                        stop=(a == RP - 1 and u + step == width),
+                        out=bank[:, first + u : first + u + count],
+                        lhsT=weights,
+                        lhsT_scale=weight_scales,
+                        rhs=zq_codes[s, a, lo + first][:, u : u + count].bitcast(FP8X4),
+                        rhs_scale=zq_scales[s, a, lo + first][:, u : u + count],
+                        start=(i == 0),
+                        stop=(i == len(passes) - 1),
                     )
-            y_t = ring.tile([P, width], F32, name="y_t", bufs=2)
+            return bank
+
+        def window(lo, n, width):
+            return out_t[n][:].indirect(offs2_t[:, lo // 16 : (lo + width) // 16])
+
+        def weigh_on_vector(lo, n, bank):
+            yw_t = ring.tile([P, CHUNK], F32, name="held", bufs=14, align_bytes=64)
+            nc.vector.scalar_tensor_tensor(
+                out=yw_t[:], in0=bank[:], scalar=c_t[:, n : n + 1], in1=wgo_t[:, lo : lo + CHUNK], op0=ALU.add, op1=ALU.mult
+            )
+            return yw_t
+
+        def predict_on_vector(lo, n, bank, between=None):
+            yw_t = weigh_on_vector(lo, n, bank)
+            if between is not None:
+                between()
+            nc.vector.tensor_copy(out=window(lo, n, CHUNK), in_=yw_t[:])
+
+        def predict_on_gpsimd(lo, n, ahead=True):
+            bank = products(lo, n, ahead=ahead)
+            y_t = ring.tile([P, CHUNK], F32, name="y_t", bufs=4, align_bytes=64)
             nc.scalar.activation(out=y_t[:], in_=bank[:], func=ACT.Identity, bias=c_t[:, n : n + 1])
-            yw_t = ring.tile([P, width], F32, name="yw_t", bufs=3)
-            nc.gpsimd.tensor_tensor(out=yw_t[:], in0=y_t[:], in1=wgo_t[:, lo:hi], op=ALU.mult)
-            nc.vector.tensor_copy(out=out_t[n][:].indirect(offs2_t[:, lo // 16 : hi // 16]), in_=yw_t[:])
+            yw_t = ring.tile([P, CHUNK], F32, name="pool_out", bufs=6, align_bytes=64)
+            nc.gpsimd.tensor_tensor(out=yw_t[:], in0=y_t[:], in1=wgo_t[:, lo : lo + CHUNK], op=ALU.mult)
+            nc.vector.tensor_copy(out=window(lo, n, CHUNK), in_=yw_t[:])
+
+        def predict_fused(lo, n, y_t, width=CHUNK, bank=None):
+            if bank is None:
+                bank = products(lo, n, width, ahead=True)
+            nc.scalar.activation(out=y_t[:], in_=bank[:], func=ACT.Identity, bias=c_t[:, n : n + 1])
+            nc.vector.tensor_tensor(out=window(lo, n, width), in0=y_t[:], in1=wgo_t[:, lo : lo + width], op=ALU.mult)
+
+        def predict_held(lo, n, bank=None):
+            y_t = ring.tile([P, CHUNK], F32, name="held", bufs=14, align_bytes=64)
+            predict_fused(lo, n, y_t, bank=bank)
 
         def store(n):
             nc.sync.dma_start(out=out[P * n : P * (n + 1), :], in_=out_t[n][:])
@@ -238,11 +325,11 @@ def tile_list_quadratic_state_prediction_kernel(
         load_wp(1, 2)
         load_wq(0)
         load_wq(1)
+        with nc.allow_non_contiguous_dma(reason="one bias value a partition"):
+            nc.sync.dma_start(out=c_t[:], in_=c.rearrange("(t p) -> p t", p=P))
         nc.sync.dma_start(out=wl_t[:].bitcast(I32), in_=wl_words.rearrange("a p n -> p a n").bitcast(I32))
         for q in range(4):
             load_wl_scales(q)
-        with nc.allow_non_contiguous_dma(reason="one bias value a partition"):
-            nc.sync.dma_start(out=c_t[:], in_=c.rearrange("(t p) -> p t", p=P))
         nc.sync.dma_start(offs2_t[:], offs2)
         load_wgo(0, 512)
         load_wgo(512, S)
@@ -252,9 +339,12 @@ def tile_list_quadratic_state_prediction_kernel(
         gather_codes(0, 0, S)
         gather_codes(1, 0, S)
         gather_scales(0, S)
-        quantise_wp(0, 0, 0)
-        quantise_wp(0, 1, 32)
-        quantise_wp(0, 2, 64)
+        cast_wp(0, 0, 0)
+        quantise_wp(0, 0)
+        cast_wp(0, 1, 32)
+        quantise_wp(0, 1)
+        cast_wp(0, 2, 64)
+        quantise_wp(0, 2)
         gather_codes(2, 0, 256)
         gather_codes(2, 256, 512)
         gather_codes(2, 512, S)
@@ -268,44 +358,105 @@ def tile_list_quadratic_state_prediction_kernel(
         nc.vector.tensor_tensor(out=quot_t[:], in0=quot_t[:], in1=root0_t[:], op=ALU.add)
         nc.vector.tensor_scalar(out=root_t[:], in0=quot_t[:], scalar1=0.5, scalar2=None, op0=ALU.mult)
         nc.vector.tensor_tensor(out=rootb_t[:], in0=root_t[:], in1=b_t[:], op=ALU.mult)
-        make_rows(0, 0, 256, z_first=True, spread=True)
-        make_rows(0, 256, 512)
-        quantise_wp(1, 0, P)
-        quantise_rows(0, 0, 256, [on_vector, on_vector], (0,))
-        quantise_wp(1, 1, P)
-        quantise_rows(0, 0, 256, [on_vector, on_vector], (1,))
-        quantise_wp(1, 2, P)
-        make_rows(0, 512, S)
-        quantise_rows(0, 256, 512, [on_vector, on_vector], (0,))
-        make_rows(1, 0, 256, spread=True)
-        quantise_wq(0, on_vector)
-        quantise_rows(0, 256, 512, [on_vector, on_vector], (1,))
-        quantise_rows(0, 512, 768, [on_vector, on_vector], (0,))
-        quantise_rows(1, 0, 256, [on_vector, on_vector])
-        quantise_wq(1, on_scalar)
-        quantise_rows(0, 512, 768, [on_vector, on_vector], (1,))
-        predict(0, 0)
-        predict(0, 1)
-        make_rows(1, 256, 512, (2, 0, 1))
-        quantise_rows(1, 256, 512, [on_scalar, on_scalar])
-        predict(0, 2)
-        predict(0, 3)
-        make_rows(1, 512, 768)
-        predict(256, 0)
-        predict(256, 1)
-        quantise_rows(1, 512, 768, [on_scalar, on_scalar])
-        predict(256, 2)
-        quantise_rows(0, 768, S, [on_scalar, on_scalar])
-        predict(256, 3)
-        make_rows(1, 768, S)
-        predict(512, 0)
-        quantise_rows(1, 768, S, [on_scalar, on_scalar])
-        predict(512, 1)
-        predict(768, 0)
-        store(0)
-        predict(768, 1)
-        store(1)
-        predict(512, 2, 512)
-        store(2)
-        predict(512, 3, 512)
+        make_rows(0, 0, range(4), spread=True)
+        second = {}
+        for ts in ((0, 1), (2, 3)):
+            for t, acc in multiply_rows(0, 256, ts).items():
+                second[t] = acc
+        read_rows(0, 256, second, (0,))
+        cast_wp(1, 0, P)
+        first_weave(0, 0)
+        quantise_wp(1, 0)
+        cast_wp(1, 1, 64)
+        first_weave(1, 0)
+        quantise_one(0, 0, 0)
+        quantise_wp(1, 1)
+        read_rows(0, 256, second, (1,), staged=(1,))
+        cast_wp(1, 2, 96)
+        quantise_one(1, 0, 0)
+        quantise_wp(1, 2, parts=2)
+        third = {}
+        for ts in ((0, 1), (2, 3)):
+            for t, acc in multiply_rows(0, 512, ts).items():
+                third[t] = acc
+        read_rows(0, 512, third, (0,), staged=(0,))
+        make_rows(1, 0, range(4), spread=True)
+        first_weave(0, 0, 256)
+        low = [grouped_tile([P, 1, 256, 4])]
+        cast_wq(0, 0, on_vector, low[0][:, 0])
+        quantise_one(0, 0, 256, early=True)
+        first_weave(0, 0, 512)
+        first_weave(0, 1)
+        quantise_wq(0, [0], low[0], "early_scales")
+        high = grouped_tile([P, RP, 256, 4])
+        for a in range(RP):
+            cast_wq(1, a, on_scalar, high[:, a])
+        quantise_one(0, 1, 0)
+        first_weave(1, 1)
+        low.append(grouped_tile([P, 1, 256, 4]))
+        cast_wq(0, 1, on_vector, low[1][:, 0])
+        quantise_one(1, 1, 0)
+        quantise_wq(0, [1], low[1], "early_scales")
+        quantise_one(0, 0, 512, early=True)
+        read_rows(0, 512, third, (1,))
+        later = multiply_rows(1, 256, (0, 1))
+        predict_on_vector(0, 0, products(0, 0, ahead=True), lambda: quantise_wq(1, [0, 1], high, "held"))
+        predict_on_gpsimd(0, 1)
+        read_rows(1, 256, later, behind_y=True)
+        predict_on_gpsimd(0, 2, ahead=False)
+        weave_beside(1, 0, 256)
+        make_rows(1, 256, (2, 3))
+        weave_pair(1, 256)
+        held = products(0, 3, ahead=True)
+        quantise_pair(1, 256)
+        quantise_one(1, 0, 256)
+        weighted = weigh_on_vector(0, 3, held)
+        rows_ahead = [multiply_rows(0, 768, ts) for ts in ((0, 1), (2, 3))]
+        later = [multiply_rows(1, 512, ts) for ts in ((0, 1), (2, 3))]
+        predict_on_vector(
+            256, 0, products(256, 0), lambda: nc.vector.tensor_copy(out=window(0, 3, CHUNK), in_=weighted[:])
+        )
+        for accs in rows_ahead:
+            read_rows(0, 768, accs)
+        predict_on_gpsimd(256, 1)
+        predict_on_gpsimd(256, 2)
+        for accs in later:
+            read_rows(1, 512, accs)
+        weave_beside(1, 0, 512, previous=256)
+        weave_beside(0, 0, 768)
+        shared = ring.tile([P, CHUNK, 4], BF16, name="pool_out", bufs=6, align_bytes=64)
+        nc.gpsimd.tensor_scalar(
+            out=shared[:, 0:64, :],
+            in0=rows[1, 0, 768][:, :, 0:64].rearrange("p t n -> p n t"),
+            scalar1=1.0,
+            scalar2=0.0,
+            op0=ALU.mult,
+            op1=ALU.add,
+        )
+        weave_pair(1, 512)
+        quantise_pair(1, 512)
+        quantise_one(1, 0, 512)
+        predict_held(256, 3)
+        make_rows(1, 768, (0, 1))
+        make_rows(1, 768, (2, 3))
+        y_t = ring.tile([P, CHUNK], F32, name="y_t", bufs=4, align_bytes=64)
+        predict_fused(512, 0, y_t, bank=products(512, 0))
+        stage["zq", 1, 0, 768] = shared
+        on_scalar(
+            out=shared[:, 64:CHUNK, :].rearrange("p (c i) t -> p c t i", i=4),
+            in_=rows[1, 0, 768][:, :, 64:CHUNK].rearrange("p t (c i) -> p c t i", i=4),
+        )
+        y_t = ring.tile([P, CHUNK], F32, name="grouped", bufs=9, align_bytes=64)
+        predict_fused(512, 1, y_t, bank=products(512, 1))
+        weave_pair(1, 768)
+        quantise_one(0, 0, 768)
+        quantise_one(1, 0, 768)
+        quantise_pair(1, 768)
+        predict_held(512, 2)
+        for n in range(3):
+            y_t = ring.tile([P, CHUNK], F32, name="y_t", bufs=4, align_bytes=64)
+            predict_fused(768, n, y_t)
+            store(n)
+        y_t = keep.tile([P, 512], F32, name="y_wide")
+        predict_fused(512, 3, y_t, 512)
         store(3)

@@ -17,10 +17,27 @@ ACT = mybir.ActivationFunctionType
 ALU = mybir.AluOpType
 
 P = 128
-KP = 3
-RP = 2
-NT = 4
+PACK = 4
+PASS = P * PACK
+KP = K // PASS
+RP = H // PASS
+NT = N // P
 CHUNK = 256
+WQ_COLS = N // 2
+Z, Q = 0, 1
+LOW, HIGH = (0, 1), (2, 3)
+
+VECTOR_SHARE = {(0, 0): 0, (0, 1): 32, (0, 2): 64, (1, 0): P, (1, 1): 64, (1, 2): 96}
+GPSIMD_TOKENS = 64
+
+RAW_TILES = 6
+STAGING_TILES = 9
+ROW_TILES = 10
+Y_TILES = 4
+GPSIMD_TILES = 6
+EARLY_TILES = 14
+LATE_TILES = 14
+BANKS = 8
 
 
 def tile_list_quadratic_state_prediction_kernel(
@@ -41,267 +58,236 @@ def tile_list_quadratic_state_prediction_kernel(
         v_scales = keep.tile([P, S], U8, name="v_scales", align_bytes=64)
         wl_t = keep.tile([P, RP, 2 * N], U8, name="wl_t", align_bytes=64)
         wlsc_t = keep.tile([P, RP, N // 4], I32, name="wlsc_t", align_bytes=64)
-        b_t = keep.tile([P, RP, 4], F32, name="b_t")
-        d_t = keep.tile([P, RP, 4], F32, name="d_t")
+        b_t = keep.tile([P, RP, PACK], F32, name="b_t")
+        d_t = keep.tile([P, RP, PACK], F32, name="d_t")
         c_t = keep.tile([P, NT], F32, name="c_t")
         wgo_t = keep.tile([P, S], F32, name="wgo_t")
         out_t = [keep.tile([P, T2], F32, name="out_t%d" % n) for n in range(NT)]
         tab_t = {}
         wp_raw = {}
         wq_raw = {}
-        wp_codes = {}
-        wp_scales = {}
-        wq_codes = {}
-        wq_scales = {}
-        zq_codes = {}
-        zq_scales = {}
+        wp_woven = {}
+        wp_mx = {}
+        wq_mx = {}
         rows = {}
-        stage = {}
+        woven = {}
+        unit_mx = {}
 
-        tab_scales_i = tab_scales.bitcast(I32)
-        wl_scales_i = wl_scales.bitcast(I32)
+        def raw_tile(shape, dtype):
+            return ring.tile(shape, dtype, name="raw", bufs=RAW_TILES, align_bytes=64)
+
+        def staging_tile(shape, dtype=BF16):
+            return ring.tile(shape, dtype, name="grouped", bufs=STAGING_TILES, align_bytes=64)
+
+        def row_tile(shape):
+            return ring.tile(shape, BF16, name="zq_rows", bufs=ROW_TILES, align_bytes=64)
+
+        def y_tile(shape, dtype=BF16):
+            return ring.tile(shape, dtype, name="y_t", bufs=Y_TILES, align_bytes=64)
+
+        def gpsimd_tile(shape, dtype):
+            return ring.tile(shape, dtype, name="pool_out", bufs=GPSIMD_TILES, align_bytes=64)
+
+        def early_tile(shape, dtype):
+            return ring.tile(shape, dtype, name="early_scales", bufs=EARLY_TILES, align_bytes=64)
+
+        def late_tile(shape, dtype):
+            return ring.tile(shape, dtype, name="held", bufs=LATE_TILES, align_bytes=64)
+
+        on_vector = nc.vector.tensor_copy
+        on_scalar = nc.scalar.copy
 
         def load_tab(g):
-            tab_t[g] = ring.tile([P, T], I32, name="raw", bufs=6, align_bytes=64)
-            nc.sync.dma_start(out=tab_t[g][:], in_=tab_words[g].rearrange("p t i -> p (t i)").bitcast(I32))
+            tab_t[g] = raw_tile([P, T], I32)
+            nc.sync.dma_start(out=tab_t[g][:], in_=tab_words[g].rearrange("p w i -> p (w i)").bitcast(I32))
 
         def load_wp(a, g):
-            wp_raw[a, g] = ring.tile([P, 4, 512], F32, name="raw", bufs=6, align_bytes=64)
+            wp_raw[a, g] = raw_tile([P, PACK, PASS], F32)
             nc.sync.dma_start(
                 out=wp_raw[a, g][:],
-                in_=wp[512 * g : 512 * (g + 1), 512 * a : 512 * (a + 1)].rearrange("(p j) c -> p j c", j=4),
+                in_=wp[PASS * g : PASS * (g + 1), PASS * a : PASS * (a + 1)].rearrange("(p j) w -> p j w", j=PACK),
             )
 
         def load_wq(a):
-            wq_raw[a] = ring.tile([P, 4, N], F32, name="raw", bufs=6, align_bytes=64)
-            nc.sync.dma_start(out=wq_raw[a][:], in_=wq[512 * a : 512 * (a + 1), :].rearrange("(p j) c -> p j c", j=4))
-
-        def load_wl_scales(q):
-            nc.sync.dma_start(
-                out=wlsc_t[32 * q : 32 * q + 4, :, :],
-                in_=wl_scales_i[:, 4 * q : 4 * q + 4, :].rearrange("a r n -> r a n"),
-            )
-
-        def load_wgo(lo, hi):
-            nc.sync.dma_start(out=wgo_t[:, lo:hi], in_=wgo[:, lo:hi])
+            wq_raw[a] = raw_tile([P, PACK, N], F32)
+            nc.sync.dma_start(out=wq_raw[a][:], in_=wq[PASS * a : PASS * (a + 1), :].rearrange("(p j) w -> p j w", j=PACK))
 
         def gather_codes(g, lo, hi):
             nc.vector.tensor_copy(
                 out=v_codes[g][:, lo:hi], in_=tab_t[g][:].bitcast(U32).indirect(offs_t[:, lo // 16 : hi // 16])
             )
 
-        def gather_scales(lo, hi):
-            nc.vector.tensor_copy(
-                out=v_scales[:, lo:hi], in_=tabsc_t[:].bitcast(U8).indirect(offs_t[:, lo // 16 : hi // 16])
-            )
-
-        on_vector = nc.vector.tensor_copy
-        on_scalar = nc.scalar.copy
-
-        def grouped_tile(shape):
-            return ring.tile(shape, BF16, name="grouped", bufs=9, align_bytes=64)
-
         def quantise(codes, scales, src):
             nc.vector.quantize_mx(out=codes.bitcast(FP8X4), scales=scales, in_=src)
 
-        def cast_wp(a, g, split):
-            grouped = grouped_tile([P, 4, P, 4])
-            dst = grouped[:].rearrange("p t m j -> p m j t")
-            src = wp_raw[a, g][:].rearrange("p j (m t) -> p m j t", t=4)
-            if split > 0:
-                on_vector(out=dst[:, 0:split], in_=src[:, 0:split])
-            if split < P:
-                on_scalar(out=dst[:, split:P], in_=src[:, split:P])
-            stage["wp", a, g] = grouped
+        def cast_wp(a, g):
+            wp_woven[a, g] = staging_tile([P, PACK, P, PACK])
+            dst = wp_woven[a, g][:].rearrange("p t m j -> p m j t")
+            src = wp_raw[a, g][:].rearrange("p j (m t) -> p m j t", t=PACK)
+            share = VECTOR_SHARE[a, g]
+            if share > 0:
+                on_vector(out=dst[:, 0:share], in_=src[:, 0:share])
+            if share < P:
+                on_scalar(out=dst[:, share:P], in_=src[:, share:P])
 
         def quantise_wp(a, g, parts=1):
-            wp_codes[a, g] = keep.tile([P, 512], U32, name="wp_codes%d%d" % (a, g), align_bytes=64)
-            wp_scales[a, g] = ring.tile([P, 512], U8, name="early_scales", bufs=14, align_bytes=64)
-            flat = stage["wp", a, g][:].rearrange("p t m j -> p (t m j)")
-            step = 512 // parts
-            for u in range(0, 512, step):
-                quantise(wp_codes[a, g][:, u : u + step], wp_scales[a, g][:, u : u + step], flat[:, 4 * u : 4 * (u + step)])
+            codes = keep.tile([P, PASS], U32, name="wp_codes%d%d" % (a, g), align_bytes=64)
+            scales = early_tile([P, PASS], U8)
+            flat = wp_woven[a, g][:].rearrange("p t m j -> p (t m j)")
+            step = PASS // parts
+            for u in range(0, PASS, step):
+                quantise(codes[:, u : u + step], scales[:, u : u + step], flat[:, PACK * u : PACK * (u + step)])
+            wp_mx[a, g] = (codes, scales)
 
         def cast_wq(h, a, copy, dst):
             copy(
-                out=dst.rearrange("p (c i) j -> p c j i", i=4),
-                in_=wq_raw[a][:, :, 256 * h : 256 * (h + 1)].rearrange("p j (c i) -> p c j i", i=4),
+                out=dst.rearrange("p (w i) j -> p w j i", i=4),
+                in_=wq_raw[a][:, :, WQ_COLS * h : WQ_COLS * (h + 1)].rearrange("p j (w i) -> p w j i", i=4),
             )
 
-        def quantise_wq(h, halves, grouped, tag):
-            codes = keep.tile([P, len(halves), 256], U32, name="wq_codes%d_%d" % (h, halves[0]), align_bytes=64)
-            scales = ring.tile([P, len(halves), 256], U8, name=tag, bufs=14, align_bytes=64)
+        def quantise_wq(h, halves, src, scale_tile):
+            codes = keep.tile([P, len(halves), WQ_COLS], U32, name="wq_codes%d_%d" % (h, halves[0]), align_bytes=64)
+            scales = scale_tile([P, len(halves), WQ_COLS], U8)
             quantise(
-                codes[:].rearrange("p a n -> p (a n)"),
-                scales[:].rearrange("p a n -> p (a n)"),
-                grouped[:].rearrange("p a n j -> p (a n j)"),
+                codes[:].rearrange("p a w -> p (a w)"),
+                scales[:].rearrange("p a w -> p (a w)"),
+                src[:].rearrange("p a w j -> p (a w j)"),
             )
             for i, a in enumerate(halves):
-                for m in range(2):
-                    wq_codes[a, 2 * h + m] = codes[:, i, P * m : P * (m + 1)]
-                    wq_scales[a, 2 * h + m] = scales[:, i, P * m : P * (m + 1)]
+                for side in range(WQ_COLS // P):
+                    cols = slice(P * side, P * (side + 1))
+                    wq_mx[a, h * WQ_COLS // P + side] = (codes[:, i, cols], scales[:, i, cols])
 
-        def multiply_rows(a, lo, ts, spread=False):
-            groups = [[t] for t in ts] if spread else [list(ts)]
-            accs = {}
+        def multiply_rows(a, lo, groups):
+            sums = {}
             for group in groups:
-                bank = psum.tile([P, len(group), CHUNK], F32, name="bank", bufs=8)
-                for v, t in enumerate(group):
+                bank = psum.tile([P, len(group), CHUNK], F32, name="bank", bufs=BANKS)
+                for place, t in enumerate(group):
                     cols = slice(P * t, P * (t + 1))
                     for g in range(KP):
+                        codes, scales = wp_mx[a, g]
                         nc.tensor.matmul_mx(
-                            out=bank[:, v, :],
-                            lhsT=wp_codes[a, g][:, cols].bitcast(FP8X4),
-                            lhsT_scale=wp_scales[a, g][:, cols],
+                            out=bank[:, place, :],
+                            lhsT=codes[:, cols].bitcast(FP8X4),
+                            lhsT_scale=scales[:, cols],
                             rhs=v_codes[g][:, lo : lo + CHUNK].bitcast(FP8X4),
                             rhs_scale=v_scales[4 * g : P, lo : lo + CHUNK],
                             start=(g == 0),
                             stop=(g == KP - 1),
                         )
-                    accs[t] = bank[:, v, :]
-            return accs
+                    sums[t] = bank[:, place, :]
+            return sums
 
-        def read_rows(a, lo, accs, which=(0, 1), staged=(), behind_y=False):
-            for s in which:
-                if (s, a, lo) in rows:
-                    continue
-                if behind_y and s == 0:
-                    rows[s, a, lo] = ring.tile([P, 4, CHUNK], BF16, name="y_t", bufs=4, align_bytes=64)
-                elif s in staged:
-                    rows[s, a, lo] = grouped_tile([P, 4, CHUNK])
-                else:
-                    rows[s, a, lo] = ring.tile([P, 4, CHUNK], BF16, name="zq_rows", bufs=10, align_bytes=64)
-            for s in which:
-                for t in sorted(accs):
-                    if s == 0:
-                        nc.scalar.activation(
-                            out=rows[0, a, lo][:, t, :], in_=accs[t], func=ACT.Identity, bias=b_t[:, a, t : t + 1]
-                        )
+        def read_rows(a, lo, sums, kinds=(Z, Q), first_tile=row_tile):
+            for kind in kinds:
+                if (kind, a, lo) not in rows:
+                    rows[kind, a, lo] = (first_tile if kind == kinds[0] else row_tile)([P, PACK, CHUNK])
+            for kind in kinds:
+                for t in sorted(sums):
+                    dst = rows[kind, a, lo][:, t, :]
+                    if kind == Z:
+                        nc.scalar.activation(out=dst, in_=sums[t], func=ACT.Identity, bias=b_t[:, a, t : t + 1])
                     else:
                         nc.scalar.activation(
-                            out=rows[1, a, lo][:, t, :],
-                            in_=accs[t],
+                            out=dst,
+                            in_=sums[t],
                             func=ACT.Square,
                             bias=rootb_t[:, a, t : t + 1],
                             scale=root_t[:, a, t : t + 1],
                         )
 
-        def make_rows(a, lo, ts, spread=False):
-            read_rows(a, lo, multiply_rows(a, lo, ts, spread))
+        def weave(copy, dst, src):
+            copy(out=dst.rearrange("p (w i) t -> p w t i", i=8), in_=src.rearrange("p t (w i) -> p w t i", i=8))
 
-        def weave(s, a, lo, copy, dst):
-            copy(
-                out=dst.rearrange("p (c i) t -> p c t i", i=4),
-                in_=rows[s, a, lo][:].rearrange("p t (c i) -> p c t i", i=4),
-            )
-
-        def weave_on_gpsimd(s, a, lo, dst):
+        def weave_on_gpsimd(dst, src):
             nc.gpsimd.tensor_scalar(
-                out=dst, in0=rows[s, a, lo][:].rearrange("p t n -> p n t"), scalar1=1.0, scalar2=0.0, op0=ALU.mult, op1=ALU.add
+                out=dst, in0=src.rearrange("p t w -> p w t"), scalar1=1.0, scalar2=0.0, op0=ALU.mult, op1=ALU.add
             )
 
-        def first_weave(s, a, lo=0):
-            stage["zq", s, a, lo] = grouped_tile([P, CHUNK, 4])
-            weave(s, a, lo, on_vector, stage["zq", s, a, lo][:])
+        def weave_unit(kind, a, lo):
+            woven[kind, a, lo] = staging_tile([P, CHUNK, PACK])
+            weave(on_vector, woven[kind, a, lo][:], rows[kind, a, lo][:])
 
-        def quantise_one(s, a, lo, early=False):
-            codes = keep.tile([P, CHUNK], U32, name="codes%d%d_%d" % (s, a, lo), align_bytes=64)
-            tag = "early_scales" if lo == 0 or early else "held"
-            scales = ring.tile([P, CHUNK], U8, name=tag, bufs=14, align_bytes=64)
-            quantise(codes[:], scales[:], stage["zq", s, a, lo][:].rearrange("p n t -> p (n t)"))
-            zq_codes[s, a, lo] = codes[:]
-            zq_scales[s, a, lo] = scales[:]
+        def quantise_unit(kind, a, lo, scale_tile):
+            codes = keep.tile([P, CHUNK], U32, name="codes%d%d_%d" % (kind, a, lo), align_bytes=64)
+            scales = scale_tile([P, CHUNK], U8)
+            quantise(codes[:], scales[:], woven[kind, a, lo][:].rearrange("p w t -> p (w t)"))
+            unit_mx[kind, a, lo] = (codes[:], scales[:])
 
-        def weave_on_scalar(s, a, lo, dst):
-            weave(s, a, lo, on_scalar, dst)
+        def weave_pair(lo):
+            pair = staging_tile([P, 2, CHUNK, PACK])
+            for kind in (Z, Q):
+                weave(on_scalar, pair[:, kind], rows[kind, 1, lo][:])
+            return pair
 
-        def weave_pair(a, lo):
-            grouped = grouped_tile([P, 2, CHUNK, 4])
-            for s in range(2):
-                weave_on_scalar(s, a, lo, grouped[:, s])
-            stage["pair", a, lo] = grouped
-
-        def weave_beside(s, a, lo, previous=None):
-            if previous is None:
-                lone = ring.tile([P, CHUNK, 4], BF16, name="pool_out", bufs=6, align_bytes=64)
-            else:
-                lone = stage["zq", s, a, previous]
-            weave_on_gpsimd(s, a, lo, lone[:])
-            stage["zq", s, a, lo] = lone
-
-        def quantise_pair(a, lo):
-            codes = keep.tile([P, 2, CHUNK], U32, name="pair_codes%d_%d" % (a, lo), align_bytes=64)
-            scales = ring.tile([P, 2, CHUNK], U8, name="held", bufs=14, align_bytes=64)
+        def quantise_pair(lo, pair):
+            codes = keep.tile([P, 2, CHUNK], U32, name="pair_codes1_%d" % lo, align_bytes=64)
+            scales = late_tile([P, 2, CHUNK], U8)
             quantise(
-                codes[:].rearrange("p s n -> p (s n)"),
-                scales[:].rearrange("p s n -> p (s n)"),
-                stage["pair", a, lo][:].rearrange("p s n t -> p (s n t)"),
+                codes[:].rearrange("p kind w -> p (kind w)"),
+                scales[:].rearrange("p kind w -> p (kind w)"),
+                pair[:].rearrange("p kind w t -> p (kind w t)"),
             )
-            for s in range(2):
-                zq_codes[s, a, lo] = codes[:, s, :]
-                zq_scales[s, a, lo] = scales[:, s, :]
+            for kind in (Z, Q):
+                unit_mx[kind, 1, lo] = (codes[:, kind, :], scales[:, kind, :])
 
-        def products(lo, n, width=CHUNK, ahead=False):
-            bank = psum.tile([P, width], F32, name="bank", bufs=8)
+        def multiply_y(lo, n, closing=(1,), width=CHUNK):
+            bank = psum.tile([P, width], F32, name="bank", bufs=BANKS)
+            passes = [(Q, a, 0, CHUNK) for a in range(RP) if a not in closing]
+            passes.extend((Z, a, u, P) for a in range(RP) for u in range(0, CHUNK, P))
+            passes.extend((Q, a, 0, CHUNK) for a in closing)
             for first in range(0, width, CHUNK):
-                wq_passes = [("wq", a, 0, CHUNK) for a in range(RP)]
-                wl_passes = [("wl", a, u, P) for a in range(RP) for u in range(0, CHUNK, P)]
-                if ahead:
-                    passes = wq_passes[:1] + wl_passes + wq_passes[1:]
-                else:
-                    passes = wl_passes + (wq_passes if lo == 0 else wq_passes[::-1])
                 for i, (kind, a, u, count) in enumerate(passes):
-                    if kind == "wq":
-                        weights = wq_codes[a, n].bitcast(FP8X4)
-                        weight_scales = wq_scales[a, n]
+                    if kind == Q:
+                        weights = wq_mx[a, n][0].bitcast(FP8X4)
+                        weight_scales = wq_mx[a, n][1]
                     else:
                         weights = wl_t[:, a, 2 * P * n : 2 * P * (n + 1)].bitcast(FP4X4)
                         weight_scales = wlsc_t[:, a, :].bitcast(U8)[:, P * n : P * (n + 1)]
-                    s = 1 if kind == "wq" else 0
+                    codes, scales = unit_mx[kind, a, lo + first]
                     nc.tensor.matmul_mx(
                         out=bank[:, first + u : first + u + count],
                         lhsT=weights,
                         lhsT_scale=weight_scales,
-                        rhs=zq_codes[s, a, lo + first][:, u : u + count].bitcast(FP8X4),
-                        rhs_scale=zq_scales[s, a, lo + first][:, u : u + count],
+                        rhs=codes[:, u : u + count].bitcast(FP8X4),
+                        rhs_scale=scales[:, u : u + count],
                         start=(i == 0),
                         stop=(i == len(passes) - 1),
                     )
             return bank
 
-        def window(lo, n, width):
+        def window(lo, n, width=CHUNK):
             return out_t[n][:].indirect(offs2_t[:, lo // 16 : (lo + width) // 16])
 
         def weigh_on_vector(lo, n, bank):
-            yw_t = ring.tile([P, CHUNK], F32, name="held", bufs=14, align_bytes=64)
+            weighted = late_tile([P, CHUNK], F32)
             nc.vector.scalar_tensor_tensor(
-                out=yw_t[:], in0=bank[:], scalar=c_t[:, n : n + 1], in1=wgo_t[:, lo : lo + CHUNK], op0=ALU.add, op1=ALU.mult
+                out=weighted[:],
+                in0=bank[:],
+                scalar=c_t[:, n : n + 1],
+                in1=wgo_t[:, lo : lo + CHUNK],
+                op0=ALU.add,
+                op1=ALU.mult,
             )
-            return yw_t
+            return weighted
 
-        def predict_on_vector(lo, n, bank, between=None):
-            yw_t = weigh_on_vector(lo, n, bank)
-            if between is not None:
-                between()
-            nc.vector.tensor_copy(out=window(lo, n, CHUNK), in_=yw_t[:])
+        def scatter(lo, n, weighted):
+            nc.vector.tensor_copy(out=window(lo, n), in_=weighted[:])
 
-        def predict_on_gpsimd(lo, n, ahead=True):
-            bank = products(lo, n, ahead=ahead)
-            y_t = ring.tile([P, CHUNK], F32, name="y_t", bufs=4, align_bytes=64)
-            nc.scalar.activation(out=y_t[:], in_=bank[:], func=ACT.Identity, bias=c_t[:, n : n + 1])
-            yw_t = ring.tile([P, CHUNK], F32, name="pool_out", bufs=6, align_bytes=64)
-            nc.gpsimd.tensor_tensor(out=yw_t[:], in0=y_t[:], in1=wgo_t[:, lo : lo + CHUNK], op=ALU.mult)
-            nc.vector.tensor_copy(out=window(lo, n, CHUNK), in_=yw_t[:])
+        def read_y(n, bank, y):
+            nc.scalar.activation(out=y[:], in_=bank[:], func=ACT.Identity, bias=c_t[:, n : n + 1])
 
-        def predict_fused(lo, n, y_t, width=CHUNK, bank=None):
-            if bank is None:
-                bank = products(lo, n, width, ahead=True)
-            nc.scalar.activation(out=y_t[:], in_=bank[:], func=ACT.Identity, bias=c_t[:, n : n + 1])
-            nc.vector.tensor_tensor(out=window(lo, n, width), in0=y_t[:], in1=wgo_t[:, lo : lo + width], op=ALU.mult)
+        def predict_with_gpsimd(lo, n, closing=(1,)):
+            bank = multiply_y(lo, n, closing)
+            y = y_tile([P, CHUNK], F32)
+            read_y(n, bank, y)
+            weighted = gpsimd_tile([P, CHUNK], F32)
+            nc.gpsimd.tensor_tensor(out=weighted[:], in0=y[:], in1=wgo_t[:, lo : lo + CHUNK], op=ALU.mult)
+            scatter(lo, n, weighted)
 
-        def predict_held(lo, n, bank=None):
-            y_t = ring.tile([P, CHUNK], F32, name="held", bufs=14, align_bytes=64)
-            predict_fused(lo, n, y_t, bank=bank)
+        def predict_fused(lo, n, y, closing=(1,), width=CHUNK):
+            read_y(n, multiply_y(lo, n, closing, width), y)
+            nc.vector.tensor_tensor(out=window(lo, n, width), in0=y[:], in1=wgo_t[:, lo : lo + width], op=ALU.mult)
 
         def store(n):
             nc.sync.dma_start(out=out[P * n : P * (n + 1), :], in_=out_t[n][:])
@@ -311,152 +297,147 @@ def tile_list_quadratic_state_prediction_kernel(
 
         load_tab(0)
         nc.sync.dma_start(offs_t[:], offs)
-        nc.scalar.dma_start(out=d_t[:], in_=d.rearrange("(a p t) -> p a t", a=RP, t=4))
-        nc.scalar.dma_start(out=b_t[:], in_=b.rearrange("(a p t) -> p a t", a=RP, t=4))
-        for q in range(4):
-            nc.scalar.dma_start(out=tabsc_t[32 * q : 32 * q + 4 * KP, :], in_=tab_scales_i[:, 4 * q : 4 * q + 4, :])
+        nc.scalar.dma_start(out=d_t[:], in_=d.rearrange("(a p t) -> p a t", a=RP, t=PACK))
+        nc.scalar.dma_start(out=b_t[:], in_=b.rearrange("(a p t) -> p a t", a=RP, t=PACK))
+        for quad in range(4):
+            nc.scalar.dma_start(
+                out=tabsc_t[32 * quad : 32 * quad + 4 * KP, :], in_=tab_scales.bitcast(I32)[:, 4 * quad : 4 * quad + 4, :]
+            )
         load_tab(1)
-        load_wp(0, 0)
-        load_wp(0, 1)
-        load_wp(0, 2)
+        for g in range(KP):
+            load_wp(0, g)
         load_tab(2)
-        load_wp(1, 0)
-        load_wp(1, 1)
-        load_wp(1, 2)
-        load_wq(0)
-        load_wq(1)
+        for g in range(KP):
+            load_wp(1, g)
+        for a in range(RP):
+            load_wq(a)
         with nc.allow_non_contiguous_dma(reason="one bias value a partition"):
-            nc.sync.dma_start(out=c_t[:], in_=c.rearrange("(t p) -> p t", p=P))
-        nc.sync.dma_start(out=wl_t[:].bitcast(I32), in_=wl_words.rearrange("a p n -> p a n").bitcast(I32))
-        for q in range(4):
-            load_wl_scales(q)
+            nc.sync.dma_start(out=c_t[:], in_=c.rearrange("(n p) -> p n", p=P))
+        nc.sync.dma_start(out=wl_t[:].bitcast(I32), in_=wl_words.rearrange("a p w -> p a w").bitcast(I32))
+        for quad in range(4):
+            nc.sync.dma_start(
+                out=wlsc_t[32 * quad : 32 * quad + 4, :, :],
+                in_=wl_scales.bitcast(I32)[:, 4 * quad : 4 * quad + 4, :].rearrange("a row w -> row a w"),
+            )
         nc.sync.dma_start(offs2_t[:], offs2)
-        load_wgo(0, 512)
-        load_wgo(512, S)
+        for lo in range(0, S, S // 2):
+            nc.sync.dma_start(out=wgo_t[:, lo : lo + S // 2], in_=wgo[:, lo : lo + S // 2])
 
         for n in range(NT):
             nc.vector.memset(out_t[n][:], 0.0)
         gather_codes(0, 0, S)
         gather_codes(1, 0, S)
-        gather_scales(0, S)
-        cast_wp(0, 0, 0)
-        quantise_wp(0, 0)
-        cast_wp(0, 1, 32)
-        quantise_wp(0, 1)
-        cast_wp(0, 2, 64)
-        quantise_wp(0, 2)
-        gather_codes(2, 0, 256)
-        gather_codes(2, 256, 512)
-        gather_codes(2, 512, S)
-        root0_t = keep.tile([P, RP, 4], F32, name="root0_t")
-        quot_t = keep.tile([P, RP, 4], F32, name="quot_t")
-        root_t = keep.tile([P, RP, 4], F32, name="root_t")
-        rootb_t = keep.tile([P, RP, 4], F32, name="rootb_t")
+        nc.vector.tensor_copy(out=v_scales[:, 0:S], in_=tabsc_t[:].bitcast(U8).indirect(offs_t[:, 0 : S // 16]))
+        for g in range(KP):
+            cast_wp(0, g)
+            quantise_wp(0, g)
+        gather_codes(2, 0, CHUNK)
+        gather_codes(2, CHUNK, 2 * CHUNK)
+        gather_codes(2, 2 * CHUNK, S)
+
+        root0_t = keep.tile([P, RP, PACK], F32, name="root0_t")
+        quot_t = keep.tile([P, RP, PACK], F32, name="quot_t")
+        root_t = keep.tile([P, RP, PACK], F32, name="root_t")
+        rootb_t = keep.tile([P, RP, PACK], F32, name="rootb_t")
         nc.scalar.activation(out=root0_t[:], in_=d_t[:], func=ACT.Sqrt)
         nc.vector.reciprocal(out=quot_t[:], in_=root0_t[:])
         nc.vector.tensor_tensor(out=quot_t[:], in0=quot_t[:], in1=d_t[:], op=ALU.mult)
         nc.vector.tensor_tensor(out=quot_t[:], in0=quot_t[:], in1=root0_t[:], op=ALU.add)
         nc.vector.tensor_scalar(out=root_t[:], in0=quot_t[:], scalar1=0.5, scalar2=None, op0=ALU.mult)
         nc.vector.tensor_tensor(out=rootb_t[:], in0=root_t[:], in1=b_t[:], op=ALU.mult)
-        make_rows(0, 0, range(4), spread=True)
-        second = {}
-        for ts in ((0, 1), (2, 3)):
-            for t, acc in multiply_rows(0, 256, ts).items():
-                second[t] = acc
-        read_rows(0, 256, second, (0,))
-        cast_wp(1, 0, P)
-        first_weave(0, 0)
+
+        lo0, lo1, lo2, lo3 = range(0, S, CHUNK)
+        apart = [(t,) for t in range(PACK)]
+
+        read_rows(0, lo0, multiply_rows(0, lo0, apart))
+        sums1 = multiply_rows(0, lo1, (LOW, HIGH))
+        read_rows(0, lo1, sums1, (Z,))
+        cast_wp(1, 0)
+        weave_unit(Z, 0, lo0)
         quantise_wp(1, 0)
-        cast_wp(1, 1, 64)
-        first_weave(1, 0)
-        quantise_one(0, 0, 0)
+        cast_wp(1, 1)
+        weave_unit(Q, 0, lo0)
+        quantise_unit(Z, 0, lo0, early_tile)
         quantise_wp(1, 1)
-        read_rows(0, 256, second, (1,), staged=(1,))
-        cast_wp(1, 2, 96)
-        quantise_one(1, 0, 0)
+        read_rows(0, lo1, sums1, (Q,), staging_tile)
+        cast_wp(1, 2)
+        quantise_unit(Q, 0, lo0, early_tile)
         quantise_wp(1, 2, parts=2)
-        third = {}
-        for ts in ((0, 1), (2, 3)):
-            for t, acc in multiply_rows(0, 512, ts).items():
-                third[t] = acc
-        read_rows(0, 512, third, (0,), staged=(0,))
-        make_rows(1, 0, range(4), spread=True)
-        first_weave(0, 0, 256)
-        low = [grouped_tile([P, 1, 256, 4])]
-        cast_wq(0, 0, on_vector, low[0][:, 0])
-        quantise_one(0, 0, 256, early=True)
-        first_weave(0, 0, 512)
-        first_weave(0, 1)
-        quantise_wq(0, [0], low[0], "early_scales")
-        high = grouped_tile([P, RP, 256, 4])
+        sums2 = multiply_rows(0, lo2, (LOW, HIGH))
+        read_rows(0, lo2, sums2, (Z,), staging_tile)
+
+        read_rows(1, lo0, multiply_rows(1, lo0, apart))
+        weave_unit(Z, 0, lo1)
+        wq_low0 = staging_tile([P, 1, WQ_COLS, PACK])
+        cast_wq(0, 0, on_vector, wq_low0[:, 0])
+        quantise_unit(Z, 0, lo1, early_tile)
+        weave_unit(Z, 0, lo2)
+        weave_unit(Z, 1, lo0)
+        quantise_wq(0, [0], wq_low0, early_tile)
+        wq_high = staging_tile([P, RP, WQ_COLS, PACK])
         for a in range(RP):
-            cast_wq(1, a, on_scalar, high[:, a])
-        quantise_one(0, 1, 0)
-        first_weave(1, 1)
-        low.append(grouped_tile([P, 1, 256, 4]))
-        cast_wq(0, 1, on_vector, low[1][:, 0])
-        quantise_one(1, 1, 0)
-        quantise_wq(0, [1], low[1], "early_scales")
-        quantise_one(0, 0, 512, early=True)
-        read_rows(0, 512, third, (1,))
-        later = multiply_rows(1, 256, (0, 1))
-        predict_on_vector(0, 0, products(0, 0, ahead=True), lambda: quantise_wq(1, [0, 1], high, "held"))
-        predict_on_gpsimd(0, 1)
-        read_rows(1, 256, later, behind_y=True)
-        predict_on_gpsimd(0, 2, ahead=False)
-        weave_beside(1, 0, 256)
-        make_rows(1, 256, (2, 3))
-        weave_pair(1, 256)
-        held = products(0, 3, ahead=True)
-        quantise_pair(1, 256)
-        quantise_one(1, 0, 256)
-        weighted = weigh_on_vector(0, 3, held)
-        rows_ahead = [multiply_rows(0, 768, ts) for ts in ((0, 1), (2, 3))]
-        later = [multiply_rows(1, 512, ts) for ts in ((0, 1), (2, 3))]
-        predict_on_vector(
-            256, 0, products(256, 0), lambda: nc.vector.tensor_copy(out=window(0, 3, CHUNK), in_=weighted[:])
-        )
-        for accs in rows_ahead:
-            read_rows(0, 768, accs)
-        predict_on_gpsimd(256, 1)
-        predict_on_gpsimd(256, 2)
-        for accs in later:
-            read_rows(1, 512, accs)
-        weave_beside(1, 0, 512, previous=256)
-        weave_beside(0, 0, 768)
-        shared = ring.tile([P, CHUNK, 4], BF16, name="pool_out", bufs=6, align_bytes=64)
-        nc.gpsimd.tensor_scalar(
-            out=shared[:, 0:64, :],
-            in0=rows[1, 0, 768][:, :, 0:64].rearrange("p t n -> p n t"),
-            scalar1=1.0,
-            scalar2=0.0,
-            op0=ALU.mult,
-            op1=ALU.add,
-        )
-        weave_pair(1, 512)
-        quantise_pair(1, 512)
-        quantise_one(1, 0, 512)
-        predict_held(256, 3)
-        make_rows(1, 768, (0, 1))
-        make_rows(1, 768, (2, 3))
-        y_t = ring.tile([P, CHUNK], F32, name="y_t", bufs=4, align_bytes=64)
-        predict_fused(512, 0, y_t, bank=products(512, 0))
-        stage["zq", 1, 0, 768] = shared
-        on_scalar(
-            out=shared[:, 64:CHUNK, :].rearrange("p (c i) t -> p c t i", i=4),
-            in_=rows[1, 0, 768][:, :, 64:CHUNK].rearrange("p t (c i) -> p c t i", i=4),
-        )
-        y_t = ring.tile([P, CHUNK], F32, name="grouped", bufs=9, align_bytes=64)
-        predict_fused(512, 1, y_t, bank=products(512, 1))
-        weave_pair(1, 768)
-        quantise_one(0, 0, 768)
-        quantise_one(1, 0, 768)
-        quantise_pair(1, 768)
-        predict_held(512, 2)
-        for n in range(3):
-            y_t = ring.tile([P, CHUNK], F32, name="y_t", bufs=4, align_bytes=64)
-            predict_fused(768, n, y_t)
+            cast_wq(1, a, on_scalar, wq_high[:, a])
+        quantise_unit(Z, 1, lo0, early_tile)
+        weave_unit(Q, 1, lo0)
+        wq_low1 = staging_tile([P, 1, WQ_COLS, PACK])
+        cast_wq(0, 1, on_vector, wq_low1[:, 0])
+        quantise_unit(Q, 1, lo0, early_tile)
+        quantise_wq(0, [1], wq_low1, early_tile)
+        quantise_unit(Z, 0, lo2, early_tile)
+        read_rows(0, lo2, sums2, (Q,))
+
+        sums_low = multiply_rows(1, lo1, (LOW,))
+        weighted = weigh_on_vector(lo0, 0, multiply_y(lo0, 0))
+        quantise_wq(1, [0, 1], wq_high, late_tile)
+        scatter(lo0, 0, weighted)
+        predict_with_gpsimd(lo0, 1)
+        read_rows(1, lo1, sums_low, first_tile=y_tile)
+        predict_with_gpsimd(lo0, 2, closing=(0, 1))
+        woven[Q, 0, lo1] = gpsimd_tile([P, CHUNK, PACK], BF16)
+        weave_on_gpsimd(woven[Q, 0, lo1][:], rows[Q, 0, lo1][:])
+        read_rows(1, lo1, multiply_rows(1, lo1, (HIGH,)))
+        pair = weave_pair(lo1)
+        held_bank = multiply_y(lo0, 3)
+        quantise_pair(lo1, pair)
+        quantise_unit(Q, 0, lo1, late_tile)
+        held = weigh_on_vector(lo0, 3, held_bank)
+
+        sums3 = [multiply_rows(0, lo3, (group,)) for group in (LOW, HIGH)]
+        sums_next = [multiply_rows(1, lo2, (group,)) for group in (LOW, HIGH)]
+        weighted = weigh_on_vector(lo1, 0, multiply_y(lo1, 0, closing=(1, 0)))
+        scatter(lo0, 3, held)
+        scatter(lo1, 0, weighted)
+        for sums in sums3:
+            read_rows(0, lo3, sums)
+        predict_with_gpsimd(lo1, 1)
+        predict_with_gpsimd(lo1, 2)
+        for sums in sums_next:
+            read_rows(1, lo2, sums)
+        woven[Q, 0, lo2] = woven[Q, 0, lo1]
+        weave_on_gpsimd(woven[Q, 0, lo2][:], rows[Q, 0, lo2][:])
+        woven[Z, 0, lo3] = gpsimd_tile([P, CHUNK, PACK], BF16)
+        weave_on_gpsimd(woven[Z, 0, lo3][:], rows[Z, 0, lo3][:])
+        woven[Q, 0, lo3] = gpsimd_tile([P, CHUNK, PACK], BF16)
+        weave_on_gpsimd(woven[Q, 0, lo3][:, 0:GPSIMD_TOKENS, :], rows[Q, 0, lo3][:, :, 0:GPSIMD_TOKENS])
+        pair = weave_pair(lo2)
+        quantise_pair(lo2, pair)
+        quantise_unit(Q, 0, lo2, late_tile)
+        predict_fused(lo1, 3, late_tile([P, CHUNK], F32))
+
+        for group in (LOW, HIGH):
+            read_rows(1, lo3, multiply_rows(1, lo3, (group,)))
+        predict_fused(lo2, 0, y_tile([P, CHUNK], F32), closing=(1, 0))
+        weave(on_scalar, woven[Q, 0, lo3][:, GPSIMD_TOKENS:CHUNK, :], rows[Q, 0, lo3][:, :, GPSIMD_TOKENS:CHUNK])
+        predict_fused(lo2, 1, staging_tile([P, CHUNK], F32), closing=(1, 0))
+        pair = weave_pair(lo3)
+        quantise_unit(Z, 0, lo3, late_tile)
+        quantise_unit(Q, 0, lo3, late_tile)
+        quantise_pair(lo3, pair)
+        predict_fused(lo2, 2, late_tile([P, CHUNK], F32))
+
+        for n in range(NT - 1):
+            predict_fused(lo3, n, y_tile([P, CHUNK], F32))
             store(n)
-        y_t = keep.tile([P, 512], F32, name="y_wide")
-        predict_fused(512, 3, y_t, 512)
-        store(3)
+        y_wide = keep.tile([P, 2 * CHUNK], F32, name="y_wide")
+        predict_fused(lo2, NT - 1, y_wide, width=2 * CHUNK)
+        store(NT - 1)

@@ -37,6 +37,7 @@ Y_TILES = 4
 GPSIMD_TILES = 6
 EARLY_TILES = 14
 LATE_TILES = 14
+DMA_ALIGN = 256
 BANKS = 8
 
 
@@ -53,16 +54,18 @@ def tile_list_quadratic_state_prediction_kernel(
         offs_t = lists.tile([P, S // 16], U16, name="offs_t")
         offs2_t = lists.tile([P, S // 16], U16, name="offs2_t")
 
-        tabsc_t = keep.tile([P, T // 4], I32, name="tabsc_t", align_bytes=64)
+        tabsc_t = keep.tile([P, T // 4], I32, name="tabsc_t", align_bytes=DMA_ALIGN)
         v_codes = [keep.tile([P, S], U32, name="v_codes%d" % g, align_bytes=64) for g in range(KP)]
         v_scales = keep.tile([P, S], U8, name="v_scales", align_bytes=64)
-        wl_t = keep.tile([P, RP, 2 * N], U8, name="wl_t", align_bytes=64)
+        wl_t = keep.tile([P, RP, 2 * N], U8, name="wl_t", align_bytes=DMA_ALIGN)
         wlsc_t = keep.tile([P, RP, N // 4], I32, name="wlsc_t", align_bytes=64)
-        b_t = keep.tile([P, RP, PACK], F32, name="b_t")
-        d_t = keep.tile([P, RP, PACK], F32, name="d_t")
+        b_block = keep.tile([P, RP, 2 * PACK], F32, name="b_block")
+        d_block = keep.tile([P, RP, 2 * PACK], F32, name="d_block")
+        b_t = b_block[:, :, 0:PACK]
+        d_t = d_block[:, :, 0:PACK]
         c_t = keep.tile([P, NT], F32, name="c_t")
-        wgo_t = keep.tile([P, S], F32, name="wgo_t")
-        out_t = [keep.tile([P, T2], F32, name="out_t%d" % n) for n in range(NT)]
+        wgo_t = keep.tile([P, S], F32, name="wgo_t", align_bytes=DMA_ALIGN)
+        out_t = [keep.tile([P, T2], F32, name="out_t%d" % n, align_bytes=DMA_ALIGN) for n in range(NT)]
         tab_t = {}
         wp_raw = {}
         wq_raw = {}
@@ -74,7 +77,7 @@ def tile_list_quadratic_state_prediction_kernel(
         unit_mx = {}
 
         def raw_tile(shape, dtype):
-            return ring.tile(shape, dtype, name="raw", bufs=RAW_TILES, align_bytes=64)
+            return ring.tile(shape, dtype, name="raw", bufs=RAW_TILES, align_bytes=DMA_ALIGN)
 
         def staging_tile(shape, dtype=BF16):
             return ring.tile(shape, dtype, name="grouped", bufs=STAGING_TILES, align_bytes=64)
@@ -297,8 +300,8 @@ def tile_list_quadratic_state_prediction_kernel(
 
         load_tab(0)
         nc.sync.dma_start(offs_t[:], offs)
-        nc.scalar.dma_start(out=d_t[:], in_=d.rearrange("(a p t) -> p a t", a=RP, t=PACK))
-        nc.scalar.dma_start(out=b_t[:], in_=b.rearrange("(a p t) -> p a t", a=RP, t=PACK))
+        nc.scalar.dma_start(out=d_t, in_=d.rearrange("(a p t) -> p a t", a=RP, t=PACK))
+        nc.scalar.dma_start(out=b_t, in_=b.rearrange("(a p t) -> p a t", a=RP, t=PACK))
         for quad in range(4):
             nc.scalar.dma_start(
                 out=tabsc_t[32 * quad : 32 * quad + 4 * KP, :], in_=tab_scales.bitcast(I32)[:, 4 * quad : 4 * quad + 4, :]
@@ -339,12 +342,12 @@ def tile_list_quadratic_state_prediction_kernel(
         quot_t = keep.tile([P, RP, PACK], F32, name="quot_t")
         root_t = keep.tile([P, RP, PACK], F32, name="root_t")
         rootb_t = keep.tile([P, RP, PACK], F32, name="rootb_t")
-        nc.scalar.activation(out=root0_t[:], in_=d_t[:], func=ACT.Sqrt)
+        nc.scalar.activation(out=root0_t[:], in_=d_t, func=ACT.Sqrt)
         nc.vector.reciprocal(out=quot_t[:], in_=root0_t[:])
-        nc.vector.tensor_tensor(out=quot_t[:], in0=quot_t[:], in1=d_t[:], op=ALU.mult)
+        nc.vector.tensor_tensor(out=quot_t[:], in0=quot_t[:], in1=d_t, op=ALU.mult)
         nc.vector.tensor_tensor(out=quot_t[:], in0=quot_t[:], in1=root0_t[:], op=ALU.add)
         nc.vector.tensor_scalar(out=root_t[:], in0=quot_t[:], scalar1=0.5, scalar2=None, op0=ALU.mult)
-        nc.vector.tensor_tensor(out=rootb_t[:], in0=root_t[:], in1=b_t[:], op=ALU.mult)
+        nc.vector.tensor_tensor(out=rootb_t[:], in0=root_t[:], in1=b_t, op=ALU.mult)
 
         lo0, lo1, lo2, lo3 = range(0, S, CHUNK)
         apart = [(t,) for t in range(PACK)]

from contextlib import ExitStack

import concourse.mybir as mybir

K, H, N, T, S, T2 = 1536, 1024, 512, 2048, 1024, 2048
FLOPS = 2 * K * H * S + 2 * 2 * H * N * S

F32 = mybir.dt.float32
BF16 = mybir.dt.bfloat16
I32 = mybir.dt.int32
U32 = mybir.dt.uint32
U16 = mybir.dt.uint16
U8 = mybir.dt.uint8
FP8X4 = mybir.dt.float8_e4m3fn_x4
FP4X4 = mybir.dt.float4_e2m1fn_x4
ACT = mybir.ActivationFunctionType
ALU = mybir.AluOpType

P = 128
PACK = 4
PASS = P * PACK
KP = K // PASS
RP = H // PASS
NT = N // P
CHUNK = 256
WQ_COLS = N // 2
Z, Q = 0, 1
LOW, HIGH = (0, 1), (2, 3)

VECTOR_SHARE = {(0, 0): 0, (0, 1): 32, (0, 2): 64, (1, 0): P, (1, 1): 64, (1, 2): 96}
GPSIMD_TOKENS = 64

RAW_TILES = 6
STAGING_TILES = 9
ROW_TILES = 10
Y_TILES = 4
GPSIMD_TILES = 6
EARLY_TILES = 14
LATE_TILES = 14
DMA_ALIGN = 256
BANKS = 8


def tile_list_quadratic_state_prediction_kernel(
    tc, tab_words, tab_scales, offs, wp, b, d, wl_words, wl_scales, wq, c, wgo, offs2, out
):
    nc = tc.nc
    with ExitStack() as ctx:
        lists = ctx.enter_context(tc.tile_pool(name="lists", bufs=1))
        keep = ctx.enter_context(tc.tile_pool(name="keep", bufs=1))
        ring = ctx.enter_context(tc.tile_pool(name="ring", bufs=1))
        psum = ctx.enter_context(tc.psum_pool(name="psum", bufs=1))

        offs_t = lists.tile([P, S // 16], U16, name="offs_t")
        offs2_t = lists.tile([P, S // 16], U16, name="offs2_t")

        tabsc_t = keep.tile([P, T // 4], I32, name="tabsc_t", align_bytes=DMA_ALIGN)
        v_codes = [keep.tile([P, S], U32, name="v_codes%d" % g, align_bytes=64) for g in range(KP)]
        v_scales = keep.tile([P, S], U8, name="v_scales", align_bytes=64)
        wl_t = keep.tile([P, RP, 2 * N], U8, name="wl_t", align_bytes=DMA_ALIGN)
        wlsc_t = keep.tile([P, RP, N // 4], I32, name="wlsc_t", align_bytes=64)
        b_block = keep.tile([P, RP, 2 * PACK], F32, name="b_block")
        d_block = keep.tile([P, RP, 2 * PACK], F32, name="d_block")
        b_t = b_block[:, :, 0:PACK]
        d_t = d_block[:, :, 0:PACK]
        c_t = keep.tile([P, NT], F32, name="c_t")
        wgo_t = keep.tile([P, S], F32, name="wgo_t", align_bytes=DMA_ALIGN)
        out_t = [keep.tile([P, T2], F32, name="out_t%d" % n, align_bytes=DMA_ALIGN) for n in range(NT)]
        tab_t = {}
        wp_raw = {}
        wq_raw = {}
        wp_woven = {}
        wp_mx = {}
        wq_mx = {}
        rows = {}
        woven = {}
        unit_mx = {}

        def raw_tile(shape, dtype):
            return ring.tile(shape, dtype, name="raw", bufs=RAW_TILES, align_bytes=DMA_ALIGN)

        def staging_tile(shape, dtype=BF16):
            return ring.tile(shape, dtype, name="grouped", bufs=STAGING_TILES, align_bytes=64)

        def row_tile(shape):
            return ring.tile(shape, BF16, name="zq_rows", bufs=ROW_TILES, align_bytes=64)

        def y_tile(shape, dtype=BF16):
            return ring.tile(shape, dtype, name="y_t", bufs=Y_TILES, align_bytes=64)

        def gpsimd_tile(shape, dtype):
            return ring.tile(shape, dtype, name="pool_out", bufs=GPSIMD_TILES, align_bytes=64)

        def early_tile(shape, dtype):
            return ring.tile(shape, dtype, name="early_scales", bufs=EARLY_TILES, align_bytes=64)

        def late_tile(shape, dtype):
            return ring.tile(shape, dtype, name="held", bufs=LATE_TILES, align_bytes=64)

        on_vector = nc.vector.tensor_copy
        on_scalar = nc.scalar.copy

        def load_tab(g):
            tab_t[g] = raw_tile([P, T], I32)
            nc.sync.dma_start(out=tab_t[g][:], in_=tab_words[g].rearrange("p w i -> p (w i)").bitcast(I32))

        def load_wp(a, g):
            wp_raw[a, g] = raw_tile([P, PACK, PASS], F32)
            nc.sync.dma_start(
                out=wp_raw[a, g][:],
                in_=wp[PASS * g : PASS * (g + 1), PASS * a : PASS * (a + 1)].rearrange("(p j) w -> p j w", j=PACK),
            )

        def load_wq(a):
            wq_raw[a] = raw_tile([P, PACK, N], F32)
            nc.sync.dma_start(out=wq_raw[a][:], in_=wq[PASS * a : PASS * (a + 1), :].rearrange("(p j) w -> p j w", j=PACK))

        def gather_codes(g, lo, hi):
            nc.vector.tensor_copy(
                out=v_codes[g][:, lo:hi], in_=tab_t[g][:].bitcast(U32).indirect(offs_t[:, lo // 16 : hi // 16])
            )

        def quantise(codes, scales, src):
            nc.vector.quantize_mx(out=codes.bitcast(FP8X4), scales=scales, in_=src)

        def cast_wp(a, g):
            wp_woven[a, g] = staging_tile([P, PACK, P, PACK])
            dst = wp_woven[a, g][:].rearrange("p t m j -> p m j t")
            src = wp_raw[a, g][:].rearrange("p j (m t) -> p m j t", t=PACK)
            share = VECTOR_SHARE[a, g]
            if share > 0:
                on_vector(out=dst[:, 0:share], in_=src[:, 0:share])
            if share < P:
                on_scalar(out=dst[:, share:P], in_=src[:, share:P])

        def quantise_wp(a, g, parts=1):
            codes = keep.tile([P, PASS], U32, name="wp_codes%d%d" % (a, g), align_bytes=64)
            scales = early_tile([P, PASS], U8)
            flat = wp_woven[a, g][:].rearrange("p t m j -> p (t m j)")
            step = PASS // parts
            for u in range(0, PASS, step):
                quantise(codes[:, u : u + step], scales[:, u : u + step], flat[:, PACK * u : PACK * (u + step)])
            wp_mx[a, g] = (codes, scales)

        def cast_wq(h, a, copy, dst):
            copy(
                out=dst.rearrange("p (w i) j -> p w j i", i=4),
                in_=wq_raw[a][:, :, WQ_COLS * h : WQ_COLS * (h + 1)].rearrange("p j (w i) -> p w j i", i=4),
            )

        def quantise_wq(h, halves, src, scale_tile):
            codes = keep.tile([P, len(halves), WQ_COLS], U32, name="wq_codes%d_%d" % (h, halves[0]), align_bytes=64)
            scales = scale_tile([P, len(halves), WQ_COLS], U8)
            quantise(
                codes[:].rearrange("p a w -> p (a w)"),
                scales[:].rearrange("p a w -> p (a w)"),
                src[:].rearrange("p a w j -> p (a w j)"),
            )
            for i, a in enumerate(halves):
                for side in range(WQ_COLS // P):
                    cols = slice(P * side, P * (side + 1))
                    wq_mx[a, h * WQ_COLS // P + side] = (codes[:, i, cols], scales[:, i, cols])

        def multiply_rows(a, lo, groups):
            sums = {}
            for group in groups:
                bank = psum.tile([P, len(group), CHUNK], F32, name="bank", bufs=BANKS)
                for place, t in enumerate(group):
                    cols = slice(P * t, P * (t + 1))
                    for g in range(KP):
                        codes, scales = wp_mx[a, g]
                        nc.tensor.matmul_mx(
                            out=bank[:, place, :],
                            lhsT=codes[:, cols].bitcast(FP8X4),
                            lhsT_scale=scales[:, cols],
                            rhs=v_codes[g][:, lo : lo + CHUNK].bitcast(FP8X4),
                            rhs_scale=v_scales[4 * g : P, lo : lo + CHUNK],
                            start=(g == 0),
                            stop=(g == KP - 1),
                        )
                    sums[t] = bank[:, place, :]
            return sums

        def read_rows(a, lo, sums, kinds=(Z, Q), first_tile=row_tile):
            for kind in kinds:
                if (kind, a, lo) not in rows:
                    rows[kind, a, lo] = (first_tile if kind == kinds[0] else row_tile)([P, PACK, CHUNK])
            for kind in kinds:
                for t in sorted(sums):
                    dst = rows[kind, a, lo][:, t, :]
                    if kind == Z:
                        nc.scalar.activation(out=dst, in_=sums[t], func=ACT.Identity, bias=b_t[:, a, t : t + 1])
                    else:
                        nc.scalar.activation(
                            out=dst,
                            in_=sums[t],
                            func=ACT.Square,
                            bias=rootb_t[:, a, t : t + 1],
                            scale=root_t[:, a, t : t + 1],
                        )

        def weave(copy, dst, src):
            copy(out=dst.rearrange("p (w i) t -> p w t i", i=8), in_=src.rearrange("p t (w i) -> p w t i", i=8))

        def weave_on_gpsimd(dst, src):
            nc.gpsimd.tensor_scalar(
                out=dst, in0=src.rearrange("p t w -> p w t"), scalar1=1.0, scalar2=0.0, op0=ALU.mult, op1=ALU.add
            )

        def weave_unit(kind, a, lo):
            woven[kind, a, lo] = staging_tile([P, CHUNK, PACK])
            weave(on_vector, woven[kind, a, lo][:], rows[kind, a, lo][:])

        def quantise_unit(kind, a, lo, scale_tile):
            codes = keep.tile([P, CHUNK], U32, name="codes%d%d_%d" % (kind, a, lo), align_bytes=64)
            scales = scale_tile([P, CHUNK], U8)
            quantise(codes[:], scales[:], woven[kind, a, lo][:].rearrange("p w t -> p (w t)"))
            unit_mx[kind, a, lo] = (codes[:], scales[:])

        def weave_pair(lo):
            pair = staging_tile([P, 2, CHUNK, PACK])
            for kind in (Z, Q):
                weave(on_scalar, pair[:, kind], rows[kind, 1, lo][:])
            return pair

        def quantise_pair(lo, pair):
            codes = keep.tile([P, 2, CHUNK], U32, name="pair_codes1_%d" % lo, align_bytes=64)
            scales = late_tile([P, 2, CHUNK], U8)
            quantise(
                codes[:].rearrange("p kind w -> p (kind w)"),
                scales[:].rearrange("p kind w -> p (kind w)"),
                pair[:].rearrange("p kind w t -> p (kind w t)"),
            )
            for kind in (Z, Q):
                unit_mx[kind, 1, lo] = (codes[:, kind, :], scales[:, kind, :])

        def multiply_y(lo, n, closing=(1,), width=CHUNK):
            bank = psum.tile([P, width], F32, name="bank", bufs=BANKS)
            passes = [(Q, a, 0, CHUNK) for a in range(RP) if a not in closing]
            passes.extend((Z, a, u, P) for a in range(RP) for u in range(0, CHUNK, P))
            passes.extend((Q, a, 0, CHUNK) for a in closing)
            for first in range(0, width, CHUNK):
                for i, (kind, a, u, count) in enumerate(passes):
                    if kind == Q:
                        weights = wq_mx[a, n][0].bitcast(FP8X4)
                        weight_scales = wq_mx[a, n][1]
                    else:
                        weights = wl_t[:, a, 2 * P * n : 2 * P * (n + 1)].bitcast(FP4X4)
                        weight_scales = wlsc_t[:, a, :].bitcast(U8)[:, P * n : P * (n + 1)]
                    codes, scales = unit_mx[kind, a, lo + first]
                    nc.tensor.matmul_mx(
                        out=bank[:, first + u : first + u + count],
                        lhsT=weights,
                        lhsT_scale=weight_scales,
                        rhs=codes[:, u : u + count].bitcast(FP8X4),
                        rhs_scale=scales[:, u : u + count],
                        start=(i == 0),
                        stop=(i == len(passes) - 1),
                    )
            return bank

        def window(lo, n, width=CHUNK):
            return out_t[n][:].indirect(offs2_t[:, lo // 16 : (lo + width) // 16])

        def weigh_on_vector(lo, n, bank):
            weighted = late_tile([P, CHUNK], F32)
            nc.vector.scalar_tensor_tensor(
                out=weighted[:],
                in0=bank[:],
                scalar=c_t[:, n : n + 1],
                in1=wgo_t[:, lo : lo + CHUNK],
                op0=ALU.add,
                op1=ALU.mult,
            )
            return weighted

        def scatter(lo, n, weighted):
            nc.vector.tensor_copy(out=window(lo, n), in_=weighted[:])

        def read_y(n, bank, y):
            nc.scalar.activation(out=y[:], in_=bank[:], func=ACT.Identity, bias=c_t[:, n : n + 1])

        def predict_with_gpsimd(lo, n, closing=(1,)):
            bank = multiply_y(lo, n, closing)
            y = y_tile([P, CHUNK], F32)
            read_y(n, bank, y)
            weighted = gpsimd_tile([P, CHUNK], F32)
            nc.gpsimd.tensor_tensor(out=weighted[:], in0=y[:], in1=wgo_t[:, lo : lo + CHUNK], op=ALU.mult)
            scatter(lo, n, weighted)

        def predict_fused(lo, n, y, closing=(1,), width=CHUNK):
            read_y(n, multiply_y(lo, n, closing, width), y)
            nc.vector.tensor_tensor(out=window(lo, n, width), in0=y[:], in1=wgo_t[:, lo : lo + width], op=ALU.mult)

        def store(n):
            nc.sync.dma_start(out=out[P * n : P * (n + 1), :], in_=out_t[n][:])

        nc.vector.memset(tabsc_t[:], 0)
        nc.vector.memset(wlsc_t[:], 0)

        load_tab(0)
        nc.sync.dma_start(offs_t[:], offs)
        nc.scalar.dma_start(out=d_t, in_=d.rearrange("(a p t) -> p a t", a=RP, t=PACK))
        nc.scalar.dma_start(out=b_t, in_=b.rearrange("(a p t) -> p a t", a=RP, t=PACK))
        for quad in range(4):
            nc.scalar.dma_start(
                out=tabsc_t[32 * quad : 32 * quad + 4 * KP, :], in_=tab_scales.bitcast(I32)[:, 4 * quad : 4 * quad + 4, :]
            )
        load_tab(1)
        for g in range(KP):
            load_wp(0, g)
        load_tab(2)
        for g in range(KP):
            load_wp(1, g)
        for a in range(RP):
            load_wq(a)
        with nc.allow_non_contiguous_dma(reason="one bias value a partition"):
            nc.sync.dma_start(out=c_t[:], in_=c.rearrange("(n p) -> p n", p=P))
        nc.sync.dma_start(out=wl_t[:].bitcast(I32), in_=wl_words.rearrange("a p w -> p a w").bitcast(I32))
        for quad in range(4):
            nc.sync.dma_start(
                out=wlsc_t[32 * quad : 32 * quad + 4, :, :],
                in_=wl_scales.bitcast(I32)[:, 4 * quad : 4 * quad + 4, :].rearrange("a row w -> row a w"),
            )
        nc.sync.dma_start(offs2_t[:], offs2)
        for lo in range(0, S, S // 2):
            nc.sync.dma_start(out=wgo_t[:, lo : lo + S // 2], in_=wgo[:, lo : lo + S // 2])

        for n in range(NT):
            nc.vector.memset(out_t[n][:], 0.0)
        gather_codes(0, 0, S)
        gather_codes(1, 0, S)
        nc.vector.tensor_copy(out=v_scales[:, 0:S], in_=tabsc_t[:].bitcast(U8).indirect(offs_t[:, 0 : S // 16]))
        for g in range(KP):
            cast_wp(0, g)
            quantise_wp(0, g)
        gather_codes(2, 0, CHUNK)
        gather_codes(2, CHUNK, 2 * CHUNK)
        gather_codes(2, 2 * CHUNK, S)

        root0_t = keep.tile([P, RP, PACK], F32, name="root0_t")
        quot_t = keep.tile([P, RP, PACK], F32, name="quot_t")
        root_t = keep.tile([P, RP, PACK], F32, name="root_t")
        rootb_t = keep.tile([P, RP, PACK], F32, name="rootb_t")
        nc.scalar.activation(out=root0_t[:], in_=d_t, func=ACT.Sqrt)
        nc.vector.reciprocal(out=quot_t[:], in_=root0_t[:])
        nc.vector.tensor_tensor(out=quot_t[:], in0=quot_t[:], in1=d_t, op=ALU.mult)
        nc.vector.tensor_tensor(out=quot_t[:], in0=quot_t[:], in1=root0_t[:], op=ALU.add)
        nc.vector.tensor_scalar(out=root_t[:], in0=quot_t[:], scalar1=0.5, scalar2=None, op0=ALU.mult)
        nc.vector.tensor_tensor(out=rootb_t[:], in0=root_t[:], in1=b_t, op=ALU.mult)

        lo0, lo1, lo2, lo3 = range(0, S, CHUNK)
        apart = [(t,) for t in range(PACK)]

        read_rows(0, lo0, multiply_rows(0, lo0, apart))
        sums1 = multiply_rows(0, lo1, (LOW, HIGH))
        read_rows(0, lo1, sums1, (Z,))
        cast_wp(1, 0)
        weave_unit(Z, 0, lo0)
        quantise_wp(1, 0)
        cast_wp(1, 1)
        weave_unit(Q, 0, lo0)
        quantise_unit(Z, 0, lo0, early_tile)
        quantise_wp(1, 1)
        read_rows(0, lo1, sums1, (Q,), staging_tile)
        cast_wp(1, 2)
        quantise_unit(Q, 0, lo0, early_tile)
        quantise_wp(1, 2, parts=2)
        sums2 = multiply_rows(0, lo2, (LOW, HIGH))
        read_rows(0, lo2, sums2, (Z,), staging_tile)

        read_rows(1, lo0, multiply_rows(1, lo0, apart))
        weave_unit(Z, 0, lo1)
        wq_low0 = staging_tile([P, 1, WQ_COLS, PACK])
        cast_wq(0, 0, on_vector, wq_low0[:, 0])
        quantise_unit(Z, 0, lo1, early_tile)
        weave_unit(Z, 0, lo2)
        weave_unit(Z, 1, lo0)
        quantise_wq(0, [0], wq_low0, early_tile)
        wq_high = staging_tile([P, RP, WQ_COLS, PACK])
        for a in range(RP):
            cast_wq(1, a, on_scalar, wq_high[:, a])
        quantise_unit(Z, 1, lo0, early_tile)
        weave_unit(Q, 1, lo0)
        wq_low1 = staging_tile([P, 1, WQ_COLS, PACK])
        cast_wq(0, 1, on_vector, wq_low1[:, 0])
        quantise_unit(Q, 1, lo0, early_tile)
        quantise_wq(0, [1], wq_low1, early_tile)
        quantise_unit(Z, 0, lo2, early_tile)
        read_rows(0, lo2, sums2, (Q,))

        sums_low = multiply_rows(1, lo1, (LOW,))
        weighted = weigh_on_vector(lo0, 0, multiply_y(lo0, 0))
        quantise_wq(1, [0, 1], wq_high, late_tile)
        scatter(lo0, 0, weighted)
        predict_with_gpsimd(lo0, 1)
        read_rows(1, lo1, sums_low, first_tile=y_tile)
        predict_with_gpsimd(lo0, 2, closing=(0, 1))
        woven[Q, 0, lo1] = gpsimd_tile([P, CHUNK, PACK], BF16)
        weave_on_gpsimd(woven[Q, 0, lo1][:], rows[Q, 0, lo1][:])
        read_rows(1, lo1, multiply_rows(1, lo1, (HIGH,)))
        pair = weave_pair(lo1)
        held_bank = multiply_y(lo0, 3)
        quantise_pair(lo1, pair)
        quantise_unit(Q, 0, lo1, late_tile)
        held = weigh_on_vector(lo0, 3, held_bank)

        sums3 = [multiply_rows(0, lo3, (group,)) for group in (LOW, HIGH)]
        sums_next = [multiply_rows(1, lo2, (group,)) for group in (LOW, HIGH)]
        weighted = weigh_on_vector(lo1, 0, multiply_y(lo1, 0, closing=(1, 0)))
        scatter(lo0, 3, held)
        scatter(lo1, 0, weighted)
        for sums in sums3:
            read_rows(0, lo3, sums)
        predict_with_gpsimd(lo1, 1)
        predict_with_gpsimd(lo1, 2)
        for sums in sums_next:
            read_rows(1, lo2, sums)
        woven[Q, 0, lo2] = woven[Q, 0, lo1]
        weave_on_gpsimd(woven[Q, 0, lo2][:], rows[Q, 0, lo2][:])
        woven[Z, 0, lo3] = gpsimd_tile([P, CHUNK, PACK], BF16)
        weave_on_gpsimd(woven[Z, 0, lo3][:], rows[Z, 0, lo3][:])
        woven[Q, 0, lo3] = gpsimd_tile([P, CHUNK, PACK], BF16)
        weave_on_gpsimd(woven[Q, 0, lo3][:, 0:GPSIMD_TOKENS, :], rows[Q, 0, lo3][:, :, 0:GPSIMD_TOKENS])
        pair = weave_pair(lo2)
        quantise_pair(lo2, pair)
        quantise_unit(Q, 0, lo2, late_tile)
        predict_fused(lo1, 3, late_tile([P, CHUNK], F32))

        for group in (LOW, HIGH):
            read_rows(1, lo3, multiply_rows(1, lo3, (group,)))
        predict_fused(lo2, 0, y_tile([P, CHUNK], F32), closing=(1, 0))
        weave(on_scalar, woven[Q, 0, lo3][:, GPSIMD_TOKENS:CHUNK, :], rows[Q, 0, lo3][:, :, GPSIMD_TOKENS:CHUNK])
        predict_fused(lo2, 1, staging_tile([P, CHUNK], F32), closing=(1, 0))
        pair = weave_pair(lo3)
        quantise_unit(Z, 0, lo3, late_tile)
        quantise_unit(Q, 0, lo3, late_tile)
        quantise_pair(lo3, pair)
        predict_fused(lo2, 2, late_tile([P, CHUNK], F32))

        for n in range(NT - 1):
            predict_fused(lo3, n, y_tile([P, CHUNK], F32))
            store(n)
        y_wide = keep.tile([P, 2 * CHUNK], F32, name="y_wide")
        predict_fused(lo2, NT - 1, y_wide, width=2 * CHUNK)
        store(NT - 1)
